import numpy as np
import ml_dtypes


def mxq(x, axis, fmt="e4m3"):
    dtype, down = {"e4m3": (ml_dtypes.float8_e4m3fn, 7), "e5m2": (ml_dtypes.float8_e5m2, 14)}[fmt]
    v = np.moveaxis(np.asarray(x, np.float32).astype(ml_dtypes.bfloat16).astype(np.float64), axis, -1)
    blocks = v.reshape(v.shape[:-1] + (-1, 32))
    amax = np.abs(blocks).max(-1, keepdims=True)
    byte = np.maximum(np.where(amax > 0, np.frexp(amax)[1] - 1 + 127, 0) - down, 1)
    scale = np.exp2(byte - 127.0)
    codes = (blocks / scale).astype(np.float32).astype(dtype).astype(np.float64)
    return np.moveaxis((codes * scale).reshape(v.shape), -1, axis)


WIDE = False


def mx_kscale(k):
    if not WIDE:
        return np.ones(k)
    levels = np.array([10, -10, 5, -5, 0])
    if k % 512:
        return np.exp2(np.random.permutation(np.resize(levels, k // 32))).repeat(32)
    a = np.empty((k // 512, 16))
    for p in range(k // 512):
        a[p, :8] = np.random.permutation(np.resize(levels, 8))
        for g in range(8):
            far = levels[np.abs(levels - a[p, g]) >= 10]
            a[p, g + 8] = far[np.random.randint(len(far))]
    return np.exp2(a.ravel()).repeat(32)


BF16 = ml_dtypes.bfloat16


def bf(x):
    return np.asarray(x, np.float32).astype(BF16)


def f64(x):
    return np.asarray(x).astype(np.float64)


E2M1 = np.array([0.0, 0.5, 1.0, 1.5, 2.0, 3.0, 4.0, 6.0, -0.0, -0.5, -1.0, -1.5, -2.0, -3.0, -4.0, -6.0])


def pack_weight(w, fmt):
    k, n = w.shape
    w = f64(bf(w)).reshape(k // 32, 32, n)
    amax = np.abs(w).max(1)
    if fmt == "e4m3":
        byte = np.frexp(amax)[1] - 1 + 127 - 7
    else:
        mant, ex = np.frexp(amax / 6.0)
        byte = np.where(mant > 0.5, ex, ex - 1) + 127
    byte = np.clip(np.where(amax > 0, byte, 1), 1, 254)
    scaled = (w * np.exp2(127.0 - byte)[:, None, :]).reshape(k, n).astype(np.float32)
    by_word = np.ascontiguousarray(scaled.reshape(k // 512, 128, 4, n).transpose(0, 1, 3, 2))
    if fmt == "e4m3":
        words = by_word.astype(ml_dtypes.float8_e4m3fn).view(np.uint8)
    else:
        c = by_word.astype(ml_dtypes.float4_e2m1fn).view(np.uint8) & 0xF
        words = c[..., 0::2] | (c[..., 1::2] << 4)
    return np.ascontiguousarray(words), np.ascontiguousarray(byte.astype(np.uint8).reshape(k // 512, 16, n))


def unpack_weight(words, scales, fmt):
    g, p, n, _ = words.shape
    if fmt == "e4m3":
        vals = np.ascontiguousarray(words).view(ml_dtypes.float8_e4m3fn).astype(np.float64)
    else:
        nib = np.empty((g, p, n, 4), np.uint8)
        nib[..., 0::2] = words & 0xF
        nib[..., 1::2] = words >> 4
        vals = E2M1[nib]
    vals = vals * np.repeat(np.exp2(scales.astype(np.float64) - 127.0), 8, axis=1)[..., None]
    return vals.transpose(0, 1, 3, 2).reshape(g * 512, n)


B, S, D, R = 1, 1024, 512, 512


def sketch_features(xq, g1q, g2q, scale):
    return (xq @ g1q) * (xq @ g2q) * scale


def draw0():
    s, t = mx_kscale(D), mx_kscale(R)
    q = bf(np.random.standard_normal((B, S, D)) * s)
    k = bf(np.random.standard_normal((B, S, D)) * s)
    g1_words, g1_scales = pack_weight(np.random.standard_normal((D, R)) / np.sqrt(D) / s[:, None], "e4m3")
    g2_words, g2_scales = pack_weight(np.random.standard_normal((D, R)) / np.sqrt(D) / s[:, None], "e4m3")
    return {
        "q": q,
        "k": k,
        "g1_words": g1_words,
        "g1_scales": g1_scales,
        "g2_words": g2_words,
        "g2_scales": g2_scales,
        "a": bf((1.0 + 0.1 * np.random.standard_normal(R)) * t),
        "b": bf((1.0 + 0.1 * np.random.standard_normal(R)) / t),
    }


def core(q, k, g1_words, g1_scales, g2_words, g2_scales, a, b):
    n = q.shape[1]
    g1q = unpack_weight(g1_words, g1_scales, "e4m3")
    g2q = unpack_weight(g2_words, g2_scales, "e4m3")
    r = g1q.shape[1]
    fq = sketch_features(mxq(f64(q), 2, "e4m3"), g1q, g2q, f64(a))
    fk = sketch_features(mxq(f64(k), 2, "e4m3"), g1q, g2q, f64(b))
    z = (mxq(fq, 2, "e4m3") @ mxq(fk, 2, "e4m3").transpose(0, 2, 1)) / np.sqrt(r)
    rows = np.arange(n)[:, None]
    cols = np.arange(n)[None, :]
    l = np.where((cols <= rows)[None, :, :], z * z, 0.0)
    den = 1.0 + (1.0 / n) * np.sum(l, axis=-1)
    return l / den[:, :, None]


def e4m3fn_bytes(y):
    return np.clip(np.asarray(y, np.float64), -448.0, 448.0).astype(np.float32).astype(ml_dtypes.float8_e4m3fn).view(np.uint8)


def e4m3fn_values(b):
    return np.asarray(b, np.uint8).view(ml_dtypes.float8_e4m3fn).astype(np.float64)


def setup_inputs():
    d = draw0()
    x0 = np.asarray(d['q']).astype(np.float64)
    s = (np.max(np.abs(x0), axis=(0, 1), keepdims=True) / 448.0).astype(np.float32)
    out = {}
    for k, v in d.items():
        if k == 'q':
            out['q_bytes'] = e4m3fn_bytes(x0 / s.astype(np.float64))
            out['q_scale'] = s
        else:
            out[k] = v
    return out


def reference(q_bytes, q_scale, k, g1_words, g1_scales, g2_words, g2_scales, a, b):
    return core(e4m3fn_values(q_bytes) * q_scale.astype(np.float64), k, g1_words, g1_scales, g2_words, g2_scales, a, b)

@@ -1,0 +1,363 @@
+from contextlib import ExitStack
+
+import concourse.mybir as mybir
+from concourse.masks import make_identity
+
+S, D, R = 1024, 512, 512
+FLOPS = 4 * 2 * S * D * R + 2 * S * S * R
+
+F32 = mybir.dt.float32
+BF16 = mybir.dt.bfloat16
+I32 = mybir.dt.int32
+U32 = mybir.dt.uint32
+U8 = mybir.dt.uint8
+FP8 = mybir.dt.float8_e4m3fn
+FP8X4 = mybir.dt.float8_e4m3fn_x4
+ALU = mybir.AluOpType
+ACT = mybir.ActivationFunctionType
+
+P = 128
+PACK = 4
+GROUP = 256
+GROUPS = S // GROUP
+BANK = 512
+ROW_TILES = S // P
+Z_SCALE = 2.0 ** -10
+PARTS = 5
+
+
+def tile_polysketchdegreefourcausalweights_w8_kernel(
+    tc, q_bytes, q_scale, k, g1_words, g1_scales, g2_words, g2_scales, a, b, out
+):
+    nc = tc.nc
+    with ExitStack() as ctx:
+        keep = ctx.enter_context(tc.tile_pool(name="keep", bufs=1))
+        work = ctx.enter_context(tc.tile_pool(name="work", bufs=3))
+        psum = ctx.enter_context(tc.psum_pool(name="psum", bufs=2))
+        ctx.enter_context(tc.manual_schedule(engines={mybir.EngineType.SP}))
+
+        def kept(name, shape, dtype):
+            return keep.tile(shape, dtype, name=name, align_bytes=64)
+
+        def shared_bank(name, shape):
+            return psum.tile(shape, F32, name=name, tag="turn" if name in ("turn_bank", "diag_bank") else "score")
+
+        ident = kept("ident", [P, P], F32)
+        pick = kept("pick", [P, 2 * PACK], BF16)
+        factor_rows = kept("factor_rows", [P, P], BF16)
+        factors = kept("factors", [P, 2 * PACK], F32)
+        scale_cols = kept("scale_cols", [P, PACK], F32)
+        scale_rows = kept("scale_rows", [P, D], F32)
+        causal = kept("causal", [P, 2 * P], F32)
+        zeros = kept("zeros", [P, S - P], F32)
+        sums = kept("sums", [P, ROW_TILES, PARTS], F32)
+        w_raw = [kept("w_raw%d" % g, [P, R], U32) for g in range(2)]
+        w_codes = [kept("w_codes%d" % g, [P, R], U32) for g in range(2)]
+        ws_raw = [kept("ws_raw%d" % g, [P, R], U8) for g in range(2)]
+        w_scales = [kept("w_scales%d" % g, [P, R], U8) for g in range(2)]
+        k_rows = [kept("k_rows%d" % g, [P, 2 * D], BF16) for g in range(GROUPS)]
+        q_raw = [kept("qbytes%d" % g, [P, 2 * D], U8) for g in range(GROUPS)]
+        q_rows = [kept("q_rows%d" % g, [P, 2 * D], BF16) for g in range(GROUPS)]
+        rows = {"k": k_rows, "q": q_rows}
+        x_codes = {x: kept("x_codes_" + x, [P, S], U32) for x in "kq"}
+        x_scales = {x: kept("x_scales_" + x, [P, S], U8) for x in "kq"}
+        f_codes = {x: kept("f_codes_" + x, [P, S], U32) for x in "kq"}
+        f_scales = {x: kept("f_scales_" + x, [P, S], U8) for x in "kq"}
+        weights = [kept("weights%d" % i, [P, P * (i + 1)], F32) for i in range(ROW_TILES)]
+        factor_col = {"k": 0, "q": PACK}
+        live = {}
+        halves = kept("halves", [P, ROW_TILES, 2], F32)
+        warm = kept("warm", [P, BANK], BF16)
+
+        def warm_up(src, count):
+            bank = shared_bank("warm_bank", [P, BANK])
+            for n in range(count):
+                nc.tensor.matmul(bank[:], lhsT=warm[:, :P], rhs=src[:, :BANK], start=True, stop=True)
+
+        def load_weight_scales(g, src, *which):
+            src_rows = src[0].bitcast(I32)
+            for r in which:
+                nc.sync.dma_start(out=ws_raw[g][r:P:32, :].bitcast(I32), in_=src_rows[r:16:4, :])
+
+        def load_weight_words(g, src):
+            nc.sync.dma_start(out=w_raw[g][:].bitcast(I32), in_=src[0].rearrange("p n t -> p (n t)").bitcast(I32))
+
+        def load_rows(dst, src, g):
+            nc.sync.dma_start(out=dst[g][:], in_=src[0, GROUP * g : GROUP * (g + 1), :].rearrange("(p j) d -> p (j d)", j=2))
+
+        def load_factor(x, src):
+            c = factor_col[x]
+            nc.sync.dma_start(
+                out=factor_rows[c : c + PACK, :].rearrange("t (b j) -> t b j", j=8),
+                in_=src.rearrange("(b t j) -> t b j", t=PACK, j=8),
+            )
+
+        def order_weight(g):
+            nc.vector.tensor_copy(
+                out=w_codes[g][:].bitcast(I32).rearrange("p (t b j) -> p t b j", t=PACK, j=8),
+                in_=w_raw[g][:].bitcast(I32).rearrange("p (b t j) -> p t b j", t=PACK, j=8),
+            )
+            nc.vector.tensor_copy(
+                out=w_scales[g][:].bitcast(I32).rearrange("p (t b j) -> p t b j", t=PACK, j=2),
+                in_=ws_raw[g][:].bitcast(I32).rearrange("p (b t j) -> p t b j", t=PACK, j=2),
+            )
+
+        def spread_scale():
+            bank = shared_bank("scale_bank", [P, PACK, P])
+            for t in range(PACK):
+                nc.tensor.transpose(bank[:, t, :], scale_cols[:, t : t + 1].to_broadcast([P, P]), ident[:])
+            nc.scalar.copy(out=scale_rows[:].rearrange("p (n t) -> p n t", t=PACK), in_=bank[:].rearrange("p t n -> p n t"))
+
+        def turn_factors():
+            bank = shared_bank("factor_bank", [P, 2 * PACK])
+            nc.tensor.matmul(bank[:], lhsT=factor_rows[:], rhs=pick[:], start=True, stop=True)
+            nc.scalar.copy(out=factors[:], in_=bank[:])
+
+        def widen(g, j):
+            cols = slice(D * j, D * (j + 1))
+            nc.vector.tensor_tensor(out=q_rows[g][:, cols], in0=q_raw[g][:, cols].bitcast(FP8), in1=scale_rows[:], op=ALU.mult)
+
+        def turn(x, g):
+            words = rows[x][g][:].bitcast(F32)
+            bank = shared_bank("turn_bank", [P, 2, 2, P])
+            for j in range(2):
+                for u in range(2):
+                    nc.tensor.transpose(bank[:, j, u, :], words[:, 256 * j + u : 256 * (j + 1) : 2], ident[:])
+            turned = work.tile([P, GROUP * PACK], BF16, name="turned", align_bytes=64, bufs=8)
+            nc.scalar.copy(
+                out=turned[:].bitcast(F32).rearrange("p (r j u) -> p r j u", j=2, u=2),
+                in_=bank[:].rearrange("p j u r -> p r j u"),
+            )
+            live["turned", x, g] = turned
+
+        def quantize(src, codes, scales, x, g):
+            cols = slice(GROUP * g, GROUP * (g + 1))
+            nc.vector.quantize_mx(out=codes[x][:, cols].bitcast(FP8X4), scales=scales[x][:, cols], in_=live[src, x, g][:])
+
+        def project(dst, g, t, x, cols):
+            w_cols = slice(P * t, P * (t + 1))
+            nc.tensor.matmul_mx(
+                dst,
+                lhsT=w_codes[g][:, w_cols].bitcast(FP8X4),
+                lhsT_scale=w_scales[g][:, w_cols],
+                rhs=x_codes[x][:, cols].bitcast(FP8X4),
+                rhs_scale=x_scales[x][:, cols],
+                start=True,
+                stop=True,
+            )
+
+        def first_projection(x, g, half):
+            if half == 0:
+                live["first", x, g] = work.tile([P, PACK, GROUP], F32, name="first", bufs=8)
+            first = live["first", x, g]
+            bank = psum.tile([P, 2, GROUP], F32, name="first_bank")
+            for e in range(2):
+                project(bank[:, e, :], 0, 2 * half + e, x, slice(GROUP * g, GROUP * (g + 1)))
+            for e in range(2):
+                t = 2 * half + e
+                c = factor_col[x] + t
+                nc.scalar.activation(out=first[:, t, :], in_=bank[:, e, :], func=ACT.Copy, scale=factors[:, c : c + 1])
+
+        def second_projection(x, g, j):
+            bank = psum.tile([P, PACK, P], F32, name="second_bank")
+            for t in range(PACK):
+                project(bank[:, t, :], 1, t, x, slice(GROUP * g + P * j, GROUP * g + P * (j + 1)))
+            live["second", x, g, j] = bank
+
+        def product(x, g, j):
+            if j == 0:
+                live["features", x, g] = work.tile([P, GROUP * PACK], BF16, name="features", align_bytes=64, bufs=8)
+            nc.vector.tensor_tensor(
+                out=live["features", x, g][:, PACK * P * j : PACK * P * (j + 1)].rearrange("p (c i t) -> p c t i", i=4, t=PACK),
+                in0=live["second", x, g, j][:].rearrange("p t (c i) -> p c t i", i=4),
+                in1=live["first", x, g][:, :, P * j : P * (j + 1)].rearrange("p t (c i) -> p c t i", i=4),
+                op=ALU.mult,
+            )
+
+        def scores(dst, i, c0, width):
+            q_cols = slice(P * i, P * (i + 1))
+            nc.tensor.matmul_mx(
+                dst,
+                lhsT=f_codes["q"][:, q_cols].bitcast(FP8X4),
+                lhsT_scale=f_scales["q"][:, q_cols],
+                rhs=f_codes["k"][:, c0 : c0 + width].bitcast(FP8X4),
+                rhs_scale=f_scales["k"][:, c0 : c0 + width],
+                start=True,
+                stop=True,
+            )
+
+        def diagonal_scores_pe(g):
+            bank = shared_bank("diag_bank", [P, 2 * P])
+            for j in range(2):
+                i = 2 * g + j
+                scores(bank[:, P * j : P * (j + 1)], i, P * i, P)
+            live["diagonal", g] = bank
+
+        def mask(g):
+            masked = work.tile([P, 2 * P], F32, name="masked", bufs=4)
+            nc.vector.tensor_tensor(out=masked[:], in0=live["diagonal", g][:], in1=causal[:], op=ALU.mult)
+            live["masked", g] = masked
+
+        def square_diagonal(i):
+            nc.scalar.activation(
+                out=weights[i][:, P * i :],
+                in_=live["masked", i // 2][:, P * (i % 2) : P * (i % 2 + 1)],
+                func=ACT.Square,
+                scale=Z_SCALE,
+                accum_out=sums[:, i, 2:3],
+            )
+
+        def square_past(i, c0):
+            width = min(BANK, P * i - c0)
+            if width > 0:
+                bank = shared_bank("score_bank", [P, BANK])
+                done = 0
+                for n in (512, 256, 128):
+                    if width - done >= n:
+                        scores(bank[:, done : done + n], i, c0 + done, n)
+                        done = done + n
+                part = 3 + c0 // BANK
+                nc.scalar.activation(
+                    out=weights[i][:, c0 : c0 + width],
+                    in_=bank[:, :width],
+                    func=ACT.Square,
+                    scale=Z_SCALE,
+                    accum_out=sums[:, i, part : part + 1],
+                )
+
+        def row_sums(g):
+            den = work.tile([P, 2], F32, name="den")
+            nc.vector.tensor_reduce(out=den[:], in_=sums[:, 2 * g : 2 * g + 2, :], axis=mybir.AxisListType.X, op=ALU.add)
+            live["den", g] = den
+
+        def invert(g):
+            inv = work.tile([P, 2], F32, name="inv")
+            nc.vector.reciprocal(out=inv[:], in_=live["den", g][:])
+            live["inv", g] = inv
+
+        def normalise(i, engine="V"):
+            col = live["inv", i // 2][:, i % 2 : i % 2 + 1]
+            if engine == "S":
+                factor = work.tile([P, 1], F32, name="factor")
+                nc.scalar.activation(out=factor[:], in_=col, func=ACT.Copy, scale=1024.0)
+                nc.scalar.activation(out=weights[i][:], in_=weights[i][:], func=ACT.Copy, scale=factor[:])
+            else:
+                eng = nc.vector if engine == "V" else nc.gpsimd
+                eng.tensor_scalar(out=weights[i][:], in0=weights[i][:], scalar1=col, scalar2=1024.0, op0=ALU.mult, op1=ALU.mult)
+            nc.sync.dma_start(out=out[0, P * i : P * (i + 1), : P * (i + 1)], in_=weights[i][:])
+
+        nc.vector.memset(warm[:], 0.0)
+        nc.gpsimd.memset(ident[:], 0.0)
+        make_identity(nc, ident[:], nomemset=True)
+        for g in range(2):
+            nc.vector.memset(ws_raw[g][:].bitcast(I32), 0)
+        nc.vector.memset(factor_rows[:], 0.0)
+        nc.vector.memset(halves[:], 0.5)
+        nc.vector.memset(sums[:], 0.0)
+        nc.scalar.activation(out=sums[:, :, 0:2], in_=halves[:], func=ACT.Square)
+        nc.vector.memset(pick[:], 0.0)
+        nc.vector.memset(causal[:], 1.0)
+        nc.vector.memset(zeros[:], 0.0)
+        nc.gpsimd.affine_select(
+            out=pick[:], in_=pick[:], pattern=[[-1, 2 * PACK]], compare_op=ALU.not_equal, fill=1.0, base=0, channel_multiplier=1
+        )
+        nc.gpsimd.affine_select(
+            out=causal[:], in_=causal[:], pattern=[[0, 2], [-1, P]], compare_op=ALU.is_ge, fill=0.0, base=0, channel_multiplier=1
+        )
+
+        nc.sync.dma_start(out=scale_cols[:], in_=q_scale[0, 0].rearrange("(p t) -> p t", t=PACK))
+        load_rows(q_raw, q_bytes, 3)
+        load_rows(k_rows, k, 0)
+        load_weight_words(0, g1_words)
+        load_factor("k", b)
+        load_factor("q", a)
+        load_weight_scales(0, g1_scales, 0, 1, 2, 3)
+        load_rows(k_rows, k, 1)
+        load_weight_words(1, g2_words)
+        load_weight_scales(1, g2_scales, 0, 1, 2, 3)
+        load_rows(k_rows, k, 2)
+        load_rows(k_rows, k, 3)
+        load_rows(q_raw, q_bytes, 2)
+        load_rows(q_raw, q_bytes, 1)
+        load_rows(q_raw, q_bytes, 0)
+        for i in range(ROW_TILES - 1):
+            nc.sync.dma_start(out=out[0, P * i : P * (i + 1), P * (i + 1) :], in_=zeros[:, : S - P * (i + 1)])
+
+        order = [("k", 0), ("q", 3), ("k", 1), ("k", 2), ("k", 3), ("q", 2), ("q", 1), ("q", 0)]
+        last = len(order) - 1
+
+        def qx(n):
+            quantize("turned", x_codes, x_scales, *order[n])
+
+        def qf(n):
+            quantize("features", f_codes, f_scales, *order[n])
+
+        def first(n):
+            first_projection(*order[n], 0)
+            first_projection(*order[n], 1)
+
+        def G(n, j):
+            second_projection(*order[n], j)
+
+        def Pr(n, j):
+            product(*order[n], j)
+
+        def T(n):
+            turn(*order[n])
+
+        eng = "VVVVVVVV"
+
+        def prepare(n):
+            if order[n][0] == "q":
+                widen(order[n][1], 0)
+                widen(order[n][1], 1)
+            T(n)
+            qx(n)
+
+        def finish(g):
+            diagonal_scores_pe(g)
+            mask(g)
+            for i in (2 * g + 1, 2 * g):
+                square_past(i, 0)
+                square_past(i, BANK)
+                square_diagonal(i)
+            row_sums(g)
+            invert(g)
+            for i in (2 * g + 1, 2 * g):
+                normalise(i, eng[i])
+
+        warm_up(warm, 2)
+        spread_scale()
+        warm_up(k_rows[0], 2)
+        turn_factors()
+        order_weight(0)
+        for n in range(3):
+            prepare(n)
+        warm_up(q_rows[order[1][1]], 2)
+        order_weight(1)
+        for n in range(2):
+            first(n)
+        seen = []
+        waiting = []
+        pending = []
+        for n in range(last + 1 + 1):
+            if n <= last:
+                G(n, 0)
+                Pr(n, 0)
+                G(n, 1)
+                Pr(n, 1)
+                qf(n)
+                seen.append(order[n])
+                if order[n][0] == "q":
+                    waiting.append(order[n][1])
+            if n + 3 <= last:
+                prepare(n + 3)
+            if n + 2 <= last:
+                first(n + 2)
+            for g in list(waiting):
+                if all(("k", h) in seen for h in range(g + 1)):
+                    waiting.remove(g)
+                    pending.append((n + 1, g))
+            for (m, g) in pending:
+                if m == n:
+                    finish(g)

@@ -23,7 +23,8 @@ GROUPS = S // GROUP
 BANK = 512
 ROW_TILES = S // P
 Z_SCALE = 2.0 ** -10
-PARTS = 5
+PARTS = 3
+EXTRA = 8
 
 
 def tile_polysketchdegreefourcausalweights_w8_kernel(
@@ -34,7 +35,7 @@ def tile_polysketchdegreefourcausalweights_w8_kernel(
         keep = ctx.enter_context(tc.tile_pool(name="keep", bufs=1))
         work = ctx.enter_context(tc.tile_pool(name="work", bufs=3))
         psum = ctx.enter_context(tc.psum_pool(name="psum", bufs=2))
-        ctx.enter_context(tc.manual_schedule(engines={mybir.EngineType.SP}))
+        ctx.enter_context(tc.manual_schedule())
 
         def kept(name, shape, dtype):
             return keep.tile(shape, dtype, name=name, align_bytes=64)
@@ -63,10 +64,13 @@ def tile_polysketchdegreefourcausalweights_w8_kernel(
         x_scales = {x: kept("x_scales_" + x, [P, S], U8) for x in "kq"}
         f_codes = {x: kept("f_codes_" + x, [P, S], U32) for x in "kq"}
         f_scales = {x: kept("f_scales_" + x, [P, S], U8) for x in "kq"}
-        weights = [kept("weights%d" % i, [P, P * (i + 1)], F32) for i in range(ROW_TILES)]
+        weights = [kept("weights%d" % i, [P, P * (i + 1) + EXTRA], F32) for i in range(ROW_TILES)]
         factor_col = {"k": 0, "q": PACK}
         live = {}
-        halves = kept("halves", [P, ROW_TILES, 2], F32)
+        sixteens = kept("sixteens", [P, ROW_TILES, EXTRA], F32)
+        masked = kept("masked", [P, ROW_TILES, P + EXTRA], F32)
+        den = kept("den", [P, ROW_TILES], F32)
+        inv = kept("inv", [P, ROW_TILES], F32)
         warm = kept("warm", [P, BANK], BF16)
 
         def warm_up(src, count):
@@ -92,11 +96,13 @@ def tile_polysketchdegreefourcausalweights_w8_kernel(
                 in_=src.rearrange("(b t j) -> t b j", t=PACK, j=8),
             )
 
-        def order_weight(g):
+        def order_words(g):
             nc.vector.tensor_copy(
                 out=w_codes[g][:].bitcast(I32).rearrange("p (t b j) -> p t b j", t=PACK, j=8),
                 in_=w_raw[g][:].bitcast(I32).rearrange("p (b t j) -> p t b j", t=PACK, j=8),
             )
+
+        def order_scales(g):
             nc.vector.tensor_copy(
                 out=w_scales[g][:].bitcast(I32).rearrange("p (t b j) -> p t b j", t=PACK, j=2),
                 in_=ws_raw[g][:].bitcast(I32).rearrange("p (b t j) -> p t b j", t=PACK, j=2),
@@ -130,9 +136,13 @@ def tile_polysketchdegreefourcausalweights_w8_kernel(
             )
             live["turned", x, g] = turned
 
-        def quantize(src, codes, scales, x, g):
-            cols = slice(GROUP * g, GROUP * (g + 1))
-            nc.vector.quantize_mx(out=codes[x][:, cols].bitcast(FP8X4), scales=scales[x][:, cols], in_=live[src, x, g][:])
+        def quantize(src, codes, scales, x, g, j0=0, count=2):
+            cols = slice(GROUP * g + P * j0, GROUP * g + P * (j0 + count))
+            nc.vector.quantize_mx(
+                out=codes[x][:, cols].bitcast(FP8X4),
+                scales=scales[x][:, cols],
+                in_=live[src, x, g][:, PACK * P * j0 : PACK * P * (j0 + count)],
+            )
 
         def project(dst, g, t, x, cols):
             w_cols = slice(P * t, P * (t + 1))
@@ -165,7 +175,7 @@ def tile_polysketchdegreefourcausalweights_w8_kernel(
             live["second", x, g, j] = bank
 
         def product(x, g, j):
-            if j == 0:
+            if ("features", x, g) not in live:
                 live["features", x, g] = work.tile([P, GROUP * PACK], BF16, name="features", align_bytes=64, bufs=8)
             nc.vector.tensor_tensor(
                 out=live["features", x, g][:, PACK * P * j : PACK * P * (j + 1)].rearrange("p (c i t) -> p c t i", i=4, t=PACK),
@@ -186,25 +196,23 @@ def tile_polysketchdegreefourcausalweights_w8_kernel(
                 stop=True,
             )
 
-        def diagonal_scores_pe(g):
-            bank = shared_bank("diag_bank", [P, 2 * P])
-            for j in range(2):
-                i = 2 * g + j
-                scores(bank[:, P * j : P * (j + 1)], i, P * i, P)
-            live["diagonal", g] = bank
+        def diagonal_scores(i0, count):
+            bank = shared_bank("diag_bank", [P, count, P])
+            for j in range(count):
+                scores(bank[:, j, :], i0 + j, P * (i0 + j), P)
+            live["diagonal", i0] = bank
 
-        def mask(g):
-            masked = work.tile([P, 2 * P], F32, name="masked", bufs=4)
-            nc.vector.tensor_tensor(out=masked[:], in0=live["diagonal", g][:], in1=causal[:], op=ALU.mult)
-            live["masked", g] = masked
+        def mask(i0, count):
+            nc.vector.tensor_tensor(
+                out=masked[:, i0 : i0 + count, :P],
+                in0=live["diagonal", i0][:],
+                in1=causal[:, : count * P].rearrange("p (j c) -> p j c", c=P),
+                op=ALU.mult,
+            )
 
         def square_diagonal(i):
             nc.scalar.activation(
-                out=weights[i][:, P * i :],
-                in_=live["masked", i // 2][:, P * (i % 2) : P * (i % 2 + 1)],
-                func=ACT.Square,
-                scale=Z_SCALE,
-                accum_out=sums[:, i, 2:3],
+                out=weights[i][:, P * i :], in_=masked[:, i, :], func=ACT.Square, scale=Z_SCALE, accum_out=sums[:, i, 0:1]
             )
 
         def square_past(i, c0):
@@ -216,7 +224,7 @@ def tile_polysketchdegreefourcausalweights_w8_kernel(
                     if width - done >= n:
                         scores(bank[:, done : done + n], i, c0 + done, n)
                         done = done + n
-                part = 3 + c0 // BANK
+                part = 1 + c0 // BANK
                 nc.scalar.activation(
                     out=weights[i][:, c0 : c0 + width],
                     in_=bank[:, :width],
@@ -225,65 +233,65 @@ def tile_polysketchdegreefourcausalweights_w8_kernel(
                     accum_out=sums[:, i, part : part + 1],
                 )
 
-        def row_sums(g):
-            den = work.tile([P, 2], F32, name="den")
-            nc.vector.tensor_reduce(out=den[:], in_=sums[:, 2 * g : 2 * g + 2, :], axis=mybir.AxisListType.X, op=ALU.add)
-            live["den", g] = den
+        def row_sums(i0, count):
+            nc.vector.tensor_reduce(out=den[:, i0 : i0 + count], in_=sums[:, i0 : i0 + count, :], axis=mybir.AxisListType.X, op=ALU.add)
 
-        def invert(g):
-            inv = work.tile([P, 2], F32, name="inv")
-            nc.vector.reciprocal(out=inv[:], in_=live["den", g][:])
-            live["inv", g] = inv
+        def invert(i0, count):
+            src = sums[:, 0, 0:1] if i0 + count == 1 else den[:, i0 : i0 + count]
+            nc.vector.reciprocal(out=inv[:, i0 : i0 + count], in_=src)
 
         def normalise(i, engine="V"):
-            col = live["inv", i // 2][:, i % 2 : i % 2 + 1]
+            col = inv[:, i : i + 1]
+            row = weights[i][:, : P * (i + 1)]
             if engine == "S":
                 factor = work.tile([P, 1], F32, name="factor")
                 nc.scalar.activation(out=factor[:], in_=col, func=ACT.Copy, scale=1024.0)
-                nc.scalar.activation(out=weights[i][:], in_=weights[i][:], func=ACT.Copy, scale=factor[:])
+                nc.scalar.activation(out=row, in_=row, func=ACT.Copy, scale=factor[:])
             else:
                 eng = nc.vector if engine == "V" else nc.gpsimd
-                eng.tensor_scalar(out=weights[i][:], in0=weights[i][:], scalar1=col, scalar2=1024.0, op0=ALU.mult, op1=ALU.mult)
-            nc.sync.dma_start(out=out[0, P * i : P * (i + 1), : P * (i + 1)], in_=weights[i][:])
+                eng.tensor_scalar(out=row, in0=row, scalar1=col, scalar2=1024.0, op0=ALU.mult, op1=ALU.mult)
 
-        nc.vector.memset(warm[:], 0.0)
-        nc.gpsimd.memset(ident[:], 0.0)
+        def store(i):
+            nc.sync.dma_start(out=out[0, P * i : P * (i + 1), : P * (i + 1)], in_=weights[i][:, : P * (i + 1)])
+
+        nc.vector.memset(ident[:], 0.0)
         make_identity(nc, ident[:], nomemset=True)
+        nc.vector.memset(warm[:], 0.0)
         for g in range(2):
             nc.vector.memset(ws_raw[g][:].bitcast(I32), 0)
         nc.vector.memset(factor_rows[:], 0.0)
-        nc.vector.memset(halves[:], 0.5)
-        nc.vector.memset(sums[:], 0.0)
-        nc.scalar.activation(out=sums[:, :, 0:2], in_=halves[:], func=ACT.Square)
         nc.vector.memset(pick[:], 0.0)
         nc.vector.memset(causal[:], 1.0)
-        nc.vector.memset(zeros[:], 0.0)
+        nc.vector.memset(sixteens[:], 16.0)
+        nc.vector.memset(sums[:], 0.0)
+        nc.scalar.activation(out=masked[:, :, P:], in_=sixteens[:], func=ACT.Square)
         nc.gpsimd.affine_select(
             out=pick[:], in_=pick[:], pattern=[[-1, 2 * PACK]], compare_op=ALU.not_equal, fill=1.0, base=0, channel_multiplier=1
         )
         nc.gpsimd.affine_select(
             out=causal[:], in_=causal[:], pattern=[[0, 2], [-1, P]], compare_op=ALU.is_ge, fill=0.0, base=0, channel_multiplier=1
         )
+        nc.vector.memset(zeros[:], 0.0)
 
         nc.sync.dma_start(out=scale_cols[:], in_=q_scale[0, 0].rearrange("(p t) -> p t", t=PACK))
-        load_rows(q_raw, q_bytes, 3)
-        load_rows(k_rows, k, 0)
+        load_rows(q_raw, q_bytes, 2)
         load_weight_words(0, g1_words)
+        load_rows(k_rows, k, 0)
+        load_rows(k_rows, k, 1)
+        load_weight_scales(0, g1_scales, 0, 1, 2, 3)
         load_factor("k", b)
         load_factor("q", a)
-        load_weight_scales(0, g1_scales, 0, 1, 2, 3)
-        load_rows(k_rows, k, 1)
+        load_rows(q_raw, q_bytes, 3)
         load_weight_words(1, g2_words)
         load_weight_scales(1, g2_scales, 0, 1, 2, 3)
-        load_rows(k_rows, k, 2)
-        load_rows(k_rows, k, 3)
-        load_rows(q_raw, q_bytes, 2)
         load_rows(q_raw, q_bytes, 1)
+        load_rows(k_rows, k, 2)
         load_rows(q_raw, q_bytes, 0)
+        load_rows(k_rows, k, 3)
         for i in range(ROW_TILES - 1):
             nc.sync.dma_start(out=out[0, P * i : P * (i + 1), P * (i + 1) :], in_=zeros[:, : S - P * (i + 1)])
 
-        order = [("k", 0), ("q", 3), ("k", 1), ("k", 2), ("k", 3), ("q", 2), ("q", 1), ("q", 0)]
+        order = [("k", 0), ("q", 2), ("k", 1), ("k", 2), ("q", 3), ("k", 3), ("q", 1), ("q", 0)]
         last = len(order) - 1
 
         def qx(n):
@@ -305,59 +313,117 @@ def tile_polysketchdegreefourcausalweights_w8_kernel(
         def T(n):
             turn(*order[n])
 
-        eng = "VVVVVVVV"
-
-        def prepare(n):
-            if order[n][0] == "q":
-                widen(order[n][1], 0)
-                widen(order[n][1], 1)
-            T(n)
-            qx(n)
-
-        def finish(g):
-            diagonal_scores_pe(g)
-            mask(g)
-            for i in (2 * g + 1, 2 * g):
-                square_past(i, 0)
-                square_past(i, BANK)
-                square_diagonal(i)
-            row_sums(g)
-            invert(g)
-            for i in (2 * g + 1, 2 * g):
-                normalise(i, eng[i])
-
+        eng = "VVVVVVSV"
         warm_up(warm, 2)
         spread_scale()
-        warm_up(k_rows[0], 2)
+        warm_up(warm, 2)
+        order_words(0)
+        T(0)
+        T(2)
+        warm_up(k_rows[1], 1)
+        widen(2, 0)
+        widen(2, 1)
+        order_scales(0)
         turn_factors()
-        order_weight(0)
-        for n in range(3):
-            prepare(n)
-        warm_up(q_rows[order[1][1]], 2)
-        order_weight(1)
-        for n in range(2):
-            first(n)
-        seen = []
-        waiting = []
-        pending = []
-        for n in range(last + 1 + 1):
-            if n <= last:
-                G(n, 0)
-                Pr(n, 0)
-                G(n, 1)
-                Pr(n, 1)
-                qf(n)
-                seen.append(order[n])
-                if order[n][0] == "q":
-                    waiting.append(order[n][1])
-            if n + 3 <= last:
-                prepare(n + 3)
-            if n + 2 <= last:
-                first(n + 2)
-            for g in list(waiting):
-                if all(("k", h) in seen for h in range(g + 1)):
-                    waiting.remove(g)
-                    pending.append((n + 1, g))
-            for (m, g) in pending:
-                if m == n:
-                    finish(g)
+        qx(0)
+        T(1)
+        first(0)
+        warm_up(q_rows[2], 1)
+        widen(3, 0)
+        qx(2)
+        order_words(1)
+        order_scales(1)
+        qx(1)
+        widen(3, 1)
+        widen(1, 0)
+        G(0, 0)
+        first(1)
+        G(0, 1)
+        fill = {0: [(1, 1), (0, 0)], 1: [(0, 1)]}
+        turns = {0: [3, 4], 1: [5, 6], 2: [7]}
+        for n in range(5):
+            for m in turns.get(n, [])[:1]:
+                T(m)
+            if n == 4:
+                diagonal_scores(4, 2)
+            first(n + 2)
+            if n == 4:
+                square_past(5, BANK)
+            Pr(n, 0)
+            G(n + 1, 0)
+            for m in turns.get(n, [])[1:]:
+                T(m)
+            if n == 3:
+                square_past(5, 0)
+                square_past(4, 0)
+            Pr(n, 1)
+            G(n + 1, 1)
+            if n == 4:
+                mask(4, 2)
+                square_diagonal(5)
+                square_diagonal(4)
+            for w in fill.get(n, []):
+                widen(*w)
+            qx(n + 3)
+            qf(n)
+        square_past(7, 0)
+        square_past(6, 0)
+        Pr(5, 0)
+        G(6, 0)
+        square_past(6, BANK)
+        Pr(5, 1)
+        G(6, 1)
+        row_sums(4, 2)
+        qf(5)
+        invert(4, 2)
+        diagonal_scores(6, 2)
+        square_past(7, BANK)
+        Pr(6, 0)
+        normalise(5, eng[5])
+        store(5)
+        mask(6, 2)
+        square_diagonal(7)
+        square_diagonal(6)
+        first(7)
+        G(7, 1)
+        Pr(6, 1)
+        G(7, 0)
+        normalise(4, eng[4])
+        store(4)
+        qf(6)
+        row_sums(6, 2)
+        diagonal_scores(2, 2)
+        invert(6, 2)
+        normalise(6, eng[6])
+        square_past(3, 0)
+        square_past(2, 0)
+        mask(2, 2)
+        normalise(7, eng[7])
+        store(7)
+        store(6)
+        Pr(7, 1)
+        square_diagonal(3)
+        square_diagonal(2)
+        Pr(7, 0)
+        quantize("features", f_codes, f_scales, "q", 0, 1, 1)
+        diagonal_scores(1, 1)
+        square_past(1, 0)
+        quantize("features", f_codes, f_scales, "q", 0, 0, 1)
+        diagonal_scores(0, 1)
+        row_sums(2, 2)
+        mask(1, 1)
+        square_diagonal(1)
+        invert(2, 2)
+        mask(0, 1)
+        square_diagonal(0)
+        normalise(3, eng[3])
+        store(3)
+        row_sums(1, 1)
+        normalise(2, eng[2])
+        store(2)
+        invert(1, 1)
+        invert(0, 1)
+        normalise(1, eng[1])
+        store(1)
+        normalise(0, eng[0])
+        store(0)

@@ -21,6 +21,10 @@ PACK = 4
 GROUP = 256
 GROUPS = S // GROUP
 BANK = 512
+SB = 5
+LS = 3
+LV = 3
+HALF = 512
 ROW_TILES = S // P
 Z_SCALE = 2.0 ** -10
 PARTS = 3
@@ -40,8 +44,11 @@ def tile_polysketchdegreefourcausalweights_w8_kernel(
         def kept(name, shape, dtype):
             return keep.tile(shape, dtype, name=name, align_bytes=64)
 
-        def shared_bank(name, shape):
-            return psum.tile(shape, F32, name=name, tag="turn" if name in ("turn_bank", "diag_bank") else "score")
+        def scalar_bank(shape):
+            return psum.tile(shape, F32, name="scalar_bank", bufs=SB)
+
+        def vector_bank(shape):
+            return psum.tile(shape, F32, name="vector_bank", bufs=8 - SB)
 
         ident = kept("ident", [P, P], F32)
         pick = kept("pick", [P, 2 * PACK], BF16)
@@ -50,16 +57,22 @@ def tile_polysketchdegreefourcausalweights_w8_kernel(
         scale_cols = kept("scale_cols", [P, PACK], F32)
         scale_rows = kept("scale_rows", [P, D], F32)
         causal = kept("causal", [P, 2 * P], F32)
-        zeros = kept("zeros", [P, S - P], F32)
+        zeros = kept("zeros", [P, 2 * P], F32)
         sums = kept("sums", [P, ROW_TILES, PARTS], F32)
         w_raw = [kept("w_raw%d" % g, [P, R], U32) for g in range(2)]
         w_codes = [kept("w_codes%d" % g, [P, R], U32) for g in range(2)]
         ws_raw = [kept("ws_raw%d" % g, [P, R], U8) for g in range(2)]
         w_scales = [kept("w_scales%d" % g, [P, R], U8) for g in range(2)]
-        k_rows = [kept("k_rows%d" % g, [P, 2 * D], BF16) for g in range(GROUPS)]
-        q_raw = [kept("qbytes%d" % g, [P, 2 * D], U8) for g in range(GROUPS)]
+        k_rows = [kept("k_rows%d" % g, [P, 2 * D], BF16) for g in range(2)]
+        k_late = kept("k_late", [P, 4 * D], BF16)
+        k_rows = [k_rows[0][:], k_rows[1][:], k_late[:, : 2 * D], k_late[:, 2 * D :]]
+        q_halves = [kept("qbytes%d" % h, [P, 4 * D], U8) for h in range(2)]
+        q_raw = [q_halves[g // 2][:, 2 * D * (g % 2) : 2 * D * (g % 2 + 1)] for g in range(GROUPS)]
         q_rows = [kept("q_rows%d" % g, [P, 2 * D], BF16) for g in range(GROUPS)]
         rows = {"k": k_rows, "q": q_rows}
+        turned = {(x, h): kept("turned_%s%d" % (x, h), [P, HALF * PACK], BF16) for x in "kq" for h in range(2)}
+        first = {(x, h): kept("first_%s%d" % (x, h), [P, PACK, HALF], F32) for x in "kq" for h in range(2)}
+        features = {(x, g): kept("features_%s%d" % (x, g), [P, GROUP * PACK], BF16) for x in "kq" for g in range(GROUPS)}
         x_codes = {x: kept("x_codes_" + x, [P, S], U32) for x in "kq"}
         x_scales = {x: kept("x_scales_" + x, [P, S], U8) for x in "kq"}
         f_codes = {x: kept("f_codes_" + x, [P, S], U32) for x in "kq"}
@@ -71,12 +84,10 @@ def tile_polysketchdegreefourcausalweights_w8_kernel(
         masked = kept("masked", [P, ROW_TILES, P + EXTRA], F32)
         den = kept("den", [P, ROW_TILES], F32)
         inv = kept("inv", [P, ROW_TILES], F32)
-        warm = kept("warm", [P, BANK], BF16)
 
-        def warm_up(src, count):
-            bank = shared_bank("warm_bank", [P, BANK])
-            for n in range(count):
-                nc.tensor.matmul(bank[:], lhsT=warm[:, :P], rhs=src[:, :BANK], start=True, stop=True)
+        def warm_up():
+            bank = vector_bank([P, 2 * P])
+            nc.tensor.matmul(bank[:], lhsT=zeros[:, :P], rhs=zeros[:], start=True, stop=True)
 
         def load_weight_scales(g, src, *which):
             src_rows = src[0].bitcast(I32)
@@ -86,8 +97,11 @@ def tile_polysketchdegreefourcausalweights_w8_kernel(
         def load_weight_words(g, src):
             nc.sync.dma_start(out=w_raw[g][:].bitcast(I32), in_=src[0].rearrange("p n t -> p (n t)").bitcast(I32))
 
-        def load_rows(dst, src, g):
-            nc.sync.dma_start(out=dst[g][:], in_=src[0, GROUP * g : GROUP * (g + 1), :].rearrange("(p j) d -> p (j d)", j=2))
+        def load_rows(dst, src, g0, count):
+            nc.sync.dma_start(
+                out=dst.rearrange("p (g c) -> p g c", g=count),
+                in_=src[0, GROUP * g0 : GROUP * (g0 + count), :].rearrange("(g p j) d -> p g (j d)", j=2, p=P),
+            )
 
         def load_factor(x, src):
             c = factor_col[x]
@@ -108,41 +122,52 @@ def tile_polysketchdegreefourcausalweights_w8_kernel(
                 in_=ws_raw[g][:].bitcast(I32).rearrange("p (b t j) -> p t b j", t=PACK, j=2),
             )
 
-        def spread_scale():
-            bank = shared_bank("scale_bank", [P, PACK, P])
+        def spread_scale_in():
+            bank = scalar_bank([P, PACK, P])
             for t in range(PACK):
                 nc.tensor.transpose(bank[:, t, :], scale_cols[:, t : t + 1].to_broadcast([P, P]), ident[:])
+            return bank
+
+        def spread_scale(bank):
             nc.scalar.copy(out=scale_rows[:].rearrange("p (n t) -> p n t", t=PACK), in_=bank[:].rearrange("p t n -> p n t"))
 
-        def turn_factors():
-            bank = shared_bank("factor_bank", [P, 2 * PACK])
+        def turn_factors_in():
+            bank = scalar_bank([P, 2 * PACK])
             nc.tensor.matmul(bank[:], lhsT=factor_rows[:], rhs=pick[:], start=True, stop=True)
+            return bank
+
+        def turn_factors(bank):
             nc.scalar.copy(out=factors[:], in_=bank[:])
 
         def widen(g, j):
             cols = slice(D * j, D * (j + 1))
             nc.vector.tensor_tensor(out=q_rows[g][:, cols], in0=q_raw[g][:, cols].bitcast(FP8), in1=scale_rows[:], op=ALU.mult)
 
-        def turn(x, g):
+        def turn_in(x, g):
             words = rows[x][g][:].bitcast(F32)
-            bank = shared_bank("turn_bank", [P, 2, 2, P])
+            bank = scalar_bank([P, 2, 2, P])
             for j in range(2):
                 for u in range(2):
                     nc.tensor.transpose(bank[:, j, u, :], words[:, 256 * j + u : 256 * (j + 1) : 2], ident[:])
-            turned = work.tile([P, GROUP * PACK], BF16, name="turned", align_bytes=64, bufs=8)
+            return bank
+
+        def turn(bank, x, g):
+            dst = turned[x, g // 2][:, GROUP * PACK * (g % 2) : GROUP * PACK * (g % 2 + 1)]
             nc.scalar.copy(
-                out=turned[:].bitcast(F32).rearrange("p (r j u) -> p r j u", j=2, u=2),
+                out=dst.bitcast(F32).rearrange("p (r j u) -> p r j u", j=2, u=2),
                 in_=bank[:].rearrange("p j u r -> p r j u"),
             )
-            live["turned", x, g] = turned
 
-        def quantize(src, codes, scales, x, g, j0=0, count=2):
-            cols = slice(GROUP * g + P * j0, GROUP * g + P * (j0 + count))
-            nc.vector.quantize_mx(
-                out=codes[x][:, cols].bitcast(FP8X4),
-                scales=scales[x][:, cols],
-                in_=live[src, x, g][:, PACK * P * j0 : PACK * P * (j0 + count)],
-            )
+        def quantize(src, codes, scales, c0):
+            cols = slice(c0, c0 + src.shape[1] // PACK)
+            nc.vector.quantize_mx(out=codes[:, cols].bitcast(FP8X4), scales=scales[:, cols], in_=src)
+
+        def quantize_rows(x, h):
+            quantize(turned[x, h][:], x_codes[x], x_scales[x], HALF * h)
+
+        def quantize_features(x, g, j0=0, count=2):
+            src = features[x, g][:, PACK * P * j0 : PACK * P * (j0 + count)]
+            quantize(src, f_codes[x], f_scales[x], GROUP * g + P * j0)
 
         def project(dst, g, t, x, cols):
             w_cols = slice(P * t, P * (t + 1))
@@ -156,31 +181,27 @@ def tile_polysketchdegreefourcausalweights_w8_kernel(
                 stop=True,
             )
 
-        def first_projection(x, g, half):
-            if half == 0:
-                live["first", x, g] = work.tile([P, PACK, GROUP], F32, name="first", bufs=8)
-            first = live["first", x, g]
-            bank = psum.tile([P, 2, GROUP], F32, name="first_bank")
-            for e in range(2):
-                project(bank[:, e, :], 0, 2 * half + e, x, slice(GROUP * g, GROUP * (g + 1)))
-            for e in range(2):
-                t = 2 * half + e
-                c = factor_col[x] + t
-                nc.scalar.activation(out=first[:, t, :], in_=bank[:, e, :], func=ACT.Copy, scale=factors[:, c : c + 1])
+        def first_projection_in(x, h, t):
+            bank = scalar_bank([P, HALF])
+            project(bank[:], 0, t, x, slice(HALF * h, HALF * (h + 1)))
+            return bank
 
-        def second_projection(x, g, j):
-            bank = psum.tile([P, PACK, P], F32, name="second_bank")
+        def first_projection(bank, x, h, t):
+            c = factor_col[x] + t
+            nc.scalar.activation(out=first[x, h][:, t, :], in_=bank[:], func=ACT.Copy, scale=factors[:, c : c + 1])
+
+        def product_in(x, g, j):
+            bank = vector_bank([P, PACK, P])
             for t in range(PACK):
                 project(bank[:, t, :], 1, t, x, slice(GROUP * g + P * j, GROUP * g + P * (j + 1)))
-            live["second", x, g, j] = bank
+            return bank
 
-        def product(x, g, j):
-            if ("features", x, g) not in live:
-                live["features", x, g] = work.tile([P, GROUP * PACK], BF16, name="features", align_bytes=64, bufs=8)
+        def product(bank, x, g, j):
+            c0 = GROUP * (g % 2) + P * j
             nc.vector.tensor_tensor(
-                out=live["features", x, g][:, PACK * P * j : PACK * P * (j + 1)].rearrange("p (c i t) -> p c t i", i=4, t=PACK),
-                in0=live["second", x, g, j][:].rearrange("p t (c i) -> p c t i", i=4),
-                in1=live["first", x, g][:, :, P * j : P * (j + 1)].rearrange("p t (c i) -> p c t i", i=4),
+                out=features[x, g][:, PACK * P * j : PACK * P * (j + 1)].rearrange("p (c i t) -> p c t i", i=4, t=PACK),
+                in0=bank[:].rearrange("p t (c i) -> p c t i", i=4),
+                in1=first[x, g // 2][:, :, c0 : c0 + P].rearrange("p t (c i) -> p c t i", i=4),
                 op=ALU.mult,
             )
 
@@ -196,16 +217,16 @@ def tile_polysketchdegreefourcausalweights_w8_kernel(
                 stop=True,
             )
 
-        def diagonal_scores(i0, count):
-            bank = shared_bank("diag_bank", [P, count, P])
+        def mask_in(i0, count):
+            bank = vector_bank([P, count, P])
             for j in range(count):
                 scores(bank[:, j, :], i0 + j, P * (i0 + j), P)
-            live["diagonal", i0] = bank
+            return bank
 
-        def mask(i0, count):
+        def mask(bank, i0, count):
             nc.vector.tensor_tensor(
                 out=masked[:, i0 : i0 + count, :P],
-                in0=live["diagonal", i0][:],
+                in0=bank[:],
                 in1=causal[:, : count * P].rearrange("p (j c) -> p j c", c=P),
                 op=ALU.mult,
             )
@@ -215,23 +236,25 @@ def tile_polysketchdegreefourcausalweights_w8_kernel(
                 out=weights[i][:, P * i :], in_=masked[:, i, :], func=ACT.Square, scale=Z_SCALE, accum_out=sums[:, i, 0:1]
             )
 
-        def square_past(i, c0):
+        def square_past_in(i, c0):
             width = min(BANK, P * i - c0)
-            if width > 0:
-                bank = shared_bank("score_bank", [P, BANK])
-                done = 0
-                for n in (512, 256, 128):
-                    if width - done >= n:
-                        scores(bank[:, done : done + n], i, c0 + done, n)
-                        done = done + n
-                part = 1 + c0 // BANK
-                nc.scalar.activation(
-                    out=weights[i][:, c0 : c0 + width],
-                    in_=bank[:, :width],
-                    func=ACT.Square,
-                    scale=Z_SCALE,
-                    accum_out=sums[:, i, part : part + 1],
-                )
+            bank = scalar_bank([P, width])
+            done = 0
+            for n in (512, 256, 128):
+                if width - done >= n:
+                    scores(bank[:, done : done + n], i, c0 + done, n)
+                    done = done + n
+            return bank
+
+        def square_past(bank, i, c0):
+            part = 1 + c0 // BANK
+            nc.scalar.activation(
+                out=weights[i][:, c0 : c0 + bank.shape[1]],
+                in_=bank[:],
+                func=ACT.Square,
+                scale=Z_SCALE,
+                accum_out=sums[:, i, part : part + 1],
+            )
 
         def row_sums(i0, count):
             nc.vector.tensor_reduce(out=den[:, i0 : i0 + count], in_=sums[:, i0 : i0 + count, :], axis=mybir.AxisListType.X, op=ALU.add)
@@ -254,176 +277,209 @@ def tile_polysketchdegreefourcausalweights_w8_kernel(
         def store(i):
             nc.sync.dma_start(out=out[0, P * i : P * (i + 1), : P * (i + 1)], in_=weights[i][:, : P * (i + 1)])
 
-        nc.vector.memset(ident[:], 0.0)
-        make_identity(nc, ident[:], nomemset=True)
-        nc.vector.memset(warm[:], 0.0)
+        nc.vector.memset(zeros[:], 0.0)
         for g in range(2):
             nc.vector.memset(ws_raw[g][:].bitcast(I32), 0)
-        nc.vector.memset(factor_rows[:], 0.0)
-        nc.vector.memset(pick[:], 0.0)
-        nc.vector.memset(causal[:], 1.0)
+        nc.vector.memset(ident[:], 0.0)
+        make_identity(nc, ident[:], nomemset=True)
+        nc.vector.memset(factor_rows[:].bitcast(I32), 0)
         nc.vector.memset(sixteens[:], 16.0)
         nc.vector.memset(sums[:], 0.0)
+        nc.vector.memset(causal[:], 1.0)
         nc.scalar.activation(out=masked[:, :, P:], in_=sixteens[:], func=ACT.Square)
-        nc.gpsimd.affine_select(
-            out=pick[:], in_=pick[:], pattern=[[-1, 2 * PACK]], compare_op=ALU.not_equal, fill=1.0, base=0, channel_multiplier=1
-        )
         nc.gpsimd.affine_select(
             out=causal[:], in_=causal[:], pattern=[[0, 2], [-1, P]], compare_op=ALU.is_ge, fill=0.0, base=0, channel_multiplier=1
         )
-        nc.vector.memset(zeros[:], 0.0)
+        nc.vector.tensor_copy(out=pick[:], in_=ident[:, : 2 * PACK])
 
         nc.sync.dma_start(out=scale_cols[:], in_=q_scale[0, 0].rearrange("(p t) -> p t", t=PACK))
-        load_rows(q_raw, q_bytes, 2)
+        load_rows(k_rows[0], k, 0, 1)
+        load_rows(k_rows[1], k, 1, 1)
+        load_rows(q_halves[1][:], q_bytes, 2, 2)
         load_weight_words(0, g1_words)
-        load_rows(k_rows, k, 0)
-        load_rows(k_rows, k, 1)
         load_weight_scales(0, g1_scales, 0, 1, 2, 3)
         load_factor("k", b)
         load_factor("q", a)
-        load_rows(q_raw, q_bytes, 3)
         load_weight_words(1, g2_words)
         load_weight_scales(1, g2_scales, 0, 1, 2, 3)
-        load_rows(q_raw, q_bytes, 1)
-        load_rows(k_rows, k, 2)
-        load_rows(q_raw, q_bytes, 0)
-        load_rows(k_rows, k, 3)
+        load_rows(q_halves[0][:], q_bytes, 0, 2)
+        load_rows(k_late[:], k, 2, 2)
         for i in range(ROW_TILES - 1):
-            nc.sync.dma_start(out=out[0, P * i : P * (i + 1), P * (i + 1) :], in_=zeros[:, : S - P * (i + 1)])
+            blocks = ROW_TILES - 1 - i
+            nc.sync.dma_start(
+                out=out[0, P * i : P * (i + 1), P * (i + 1) :].rearrange("p (n c) -> p n c", c=P),
+                in_=zeros[:, :P].unsqueeze(1).to_broadcast([P, blocks, P]),
+            )
+        steps = [
+            (warm_up,),
+            (spread_scale,),
+            (warm_up,),
+            (turn, "k", 0),
+            (turn, "k", 1),
+            (warm_up,),
+            (widen, 2, 0),
+            (widen, 2, 1),
+            (order_words, 0),
+            (order_scales, 0),
+            (turn, "q", 2),
+            (turn_factors,),
+            (warm_up,),
+            (quantize_rows, "k", 0),
+            (first_projection, "k", 0, 0),
+            (first_projection, "k", 0, 1),
+            (widen, 3, 0),
+            (widen, 3, 1),
+            (turn, "q", 3),
+            (first_projection, "k", 0, 2),
+            (order_words, 1),
+            (order_scales, 1),
+            (widen, 1, 0),
+            (first_projection, "k", 0, 3),
+            (widen, 1, 1),
+            (widen, 0, 0),
+            (quantize_rows, "q", 1),
+            (turn, "k", 2),
+            (turn, "k", 3),
+            (first_projection, "q", 1, 0),
+            (first_projection, "q", 1, 1),
+            (widen, 0, 1),
+            (product, "k", 0, 0),
+            (product, "k", 0, 1),
+            (turn, "q", 1),
+            (first_projection, "q", 1, 2),
+            (first_projection, "q", 1, 3),
+            (quantize_rows, "k", 1),
+            (quantize_features, "k", 0, 0, 2),
+            (turn, "q", 0),
+            (product, "k", 1, 0),
+            (first_projection, "k", 1, 0),
+            (first_projection, "k", 1, 1),
+            (product, "k", 1, 1),
+            (product, "q", 2, 0),
+            (first_projection, "k", 1, 2),
+            (quantize_rows, "q", 0),
+            (product, "q", 2, 1),
+            (first_projection, "k", 1, 3),
+            (quantize_features, "k", 1, 0, 2),
+            (quantize_features, "q", 2, 0, 2),
+            (first_projection, "q", 0, 0),
+            (first_projection, "q", 0, 1),
+            (product, "q", 3, 0),
+            (first_projection, "q", 0, 2),
+            (product, "q", 3, 1),
+            (first_projection, "q", 0, 3),
+            (square_past, 5, 0),
+            (product, "k", 2, 0),
+            (square_past, 4, 0),
+            (quantize_features, "q", 3, 0, 2),
+            (product, "k", 2, 1),
+            (square_past, 7, 0),
+            (product, "k", 3, 0),
+            (quantize_features, "k", 2, 0, 2),
+            (square_past, 5, BANK),
+            (product, "k", 3, 1),
+            (mask, 4, 2),
+            (square_diagonal, 5),
+            (square_diagonal, 4),
+            (square_past, 6, 0),
+            (quantize_features, "k", 3, 0, 2),
+            (square_past, 6, BANK),
+            (product, "q", 1, 0),
+            (square_past, 7, BANK),
+            (row_sums, 4, 2),
+            (mask, 6, 2),
+            (invert, 4, 2),
+            (square_diagonal, 7),
+            (square_diagonal, 6),
+            (product, "q", 1, 1),
+            (normalise, 5, "V"),
+            (store, 5),
+            (quantize_features, "q", 1, 0, 2),
+            (square_past, 3, 0),
+            (square_past, 2, 0),
+            (row_sums, 6, 2),
+            (normalise, 4, "V"),
+            (store, 4),
+            (invert, 6, 2),
+            (product, "q", 0, 1),
+            (mask, 2, 2),
+            (square_diagonal, 3),
+            (square_diagonal, 2),
+            (normalise, 7, "V"),
+            (store, 7),
+            (normalise, 6, "S"),
+            (product, "q", 0, 0),
+            (quantize_features, "q", 0, 1, 1),
+            (row_sums, 2, 2),
+            (quantize_features, "q", 0, 0, 1),
+            (store, 6),
+            (square_past, 1, 0),
+            (invert, 2, 2),
+            (mask, 1, 1),
+            (square_diagonal, 1),
+            (mask, 0, 1),
+            (square_diagonal, 0),
+            (normalise, 3, "V"),
+            (store, 3),
+            (row_sums, 1, 1),
+            (normalise, 2, "V"),
+            (store, 2),
+            (invert, 1, 1),
+            (invert, 0, 1),
+            (normalise, 1, "V"),
+            (store, 1),
+            (normalise, 0, "V"),
+            (store, 0),
+        ]
+        fillers = {
+            spread_scale: (spread_scale_in, LS),
+            turn_factors: (turn_factors_in, LS),
+            turn: (turn_in, LS),
+            first_projection: (first_projection_in, LS),
+            square_past: (square_past_in, LS),
+            product: (product_in, LV),
+            mask: (mask_in, LV),
+        }
 
-        order = [("k", 0), ("q", 2), ("k", 1), ("k", 2), ("q", 3), ("k", 3), ("q", 1), ("q", 0)]
-        last = len(order) - 1
+        def needs(step):
+            f, args = step[0], step[1:]
+            if f == turn and args[0] == "q":
+                return [(widen, args[1], 0), (widen, args[1], 1)]
+            if f == first_projection:
+                return [(quantize_rows, args[0], args[1]), (order_scales, 0)]
+            if f == product:
+                return [(quantize_rows, args[0], args[1] // 2), (order_scales, 1)]
+            if f == square_past:
+                last_tile = min(args[0], (args[1] + BANK) // P) - 1
+                return [("q", args[0]), ("k", last_tile)]
+            if f == mask:
+                return [(x, i) for x in "qk" for i in range(args[0], args[0] + args[1])]
+            return []
 
-        def qx(n):
-            quantize("turned", x_codes, x_scales, *order[n])
-
-        def qf(n):
-            quantize("features", f_codes, f_scales, *order[n])
-
-        def first(n):
-            first_projection(*order[n], 0)
-            first_projection(*order[n], 1)
-
-        def G(n, j):
-            second_projection(*order[n], j)
-
-        def Pr(n, j):
-            product(*order[n], j)
-
-        def T(n):
-            turn(*order[n])
-
-        eng = "VVVVVVSV"
-        warm_up(warm, 2)
-        spread_scale()
-        warm_up(warm, 2)
-        order_words(0)
-        T(0)
-        T(2)
-        warm_up(k_rows[1], 1)
-        widen(2, 0)
-        widen(2, 1)
-        order_scales(0)
-        turn_factors()
-        qx(0)
-        T(1)
-        first(0)
-        warm_up(q_rows[2], 1)
-        widen(3, 0)
-        qx(2)
-        order_words(1)
-        order_scales(1)
-        qx(1)
-        widen(3, 1)
-        widen(1, 0)
-        G(0, 0)
-        first(1)
-        G(0, 1)
-        fill = {0: [(1, 1), (0, 0)], 1: [(0, 1)]}
-        turns = {0: [3, 4], 1: [5, 6], 2: [7]}
-        for n in range(5):
-            for m in turns.get(n, [])[:1]:
-                T(m)
-            if n == 4:
-                diagonal_scores(4, 2)
-            first(n + 2)
-            if n == 4:
-                square_past(5, BANK)
-            Pr(n, 0)
-            G(n + 1, 0)
-            for m in turns.get(n, [])[1:]:
-                T(m)
-            if n == 3:
-                square_past(5, 0)
-                square_past(4, 0)
-            Pr(n, 1)
-            G(n + 1, 1)
-            if n == 4:
-                mask(4, 2)
-                square_diagonal(5)
-                square_diagonal(4)
-            for w in fill.get(n, []):
-                widen(*w)
-            qx(n + 3)
-            qf(n)
-        square_past(7, 0)
-        square_past(6, 0)
-        Pr(5, 0)
-        G(6, 0)
-        square_past(6, BANK)
-        Pr(5, 1)
-        G(6, 1)
-        row_sums(4, 2)
-        qf(5)
-        invert(4, 2)
-        diagonal_scores(6, 2)
-        square_past(7, BANK)
-        Pr(6, 0)
-        normalise(5, eng[5])
-        store(5)
-        mask(6, 2)
-        square_diagonal(7)
-        square_diagonal(6)
-        first(7)
-        G(7, 1)
-        Pr(6, 1)
-        G(7, 0)
-        normalise(4, eng[4])
-        store(4)
-        qf(6)
-        row_sums(6, 2)
-        diagonal_scores(2, 2)
-        invert(6, 2)
-        normalise(6, eng[6])
-        square_past(3, 0)
-        square_past(2, 0)
-        mask(2, 2)
-        normalise(7, eng[7])
-        store(7)
-        store(6)
-        Pr(7, 1)
-        square_diagonal(3)
-        square_diagonal(2)
-        Pr(7, 0)
-        quantize("features", f_codes, f_scales, "q", 0, 1, 1)
-        diagonal_scores(1, 1)
-        square_past(1, 0)
-        quantize("features", f_codes, f_scales, "q", 0, 0, 1)
-        diagonal_scores(0, 1)
-        row_sums(2, 2)
-        mask(1, 1)
-        square_diagonal(1)
-        invert(2, 2)
-        mask(0, 1)
-        square_diagonal(0)
-        normalise(3, eng[3])
-        store(3)
-        row_sums(1, 1)
-        normalise(2, eng[2])
-        store(2)
-        invert(1, 1)
-        invert(0, 1)
-        normalise(1, eng[1])
-        store(1)
-        normalise(0, eng[0])
-        store(0)
+        done = set()
+        banks = {}
+        streams = {reader: [s for s in steps if s[0] in fillers and (s[0] in (product, mask)) == (reader == "vector")] for reader in ("scalar", "vector")}
+        read = {"scalar": 0, "vector": 0}
+        filled = {"scalar": 0, "vector": 0}
+        for at, step in enumerate(steps):
+            horizon = min([n for n in range(at, len(steps)) if steps[n] == (warm_up,)] + [len(steps)])
+            ahead = []
+            for reader in streams:
+                items = streams[reader]
+                n = filled[reader]
+                while n < len(items) and steps.index(items[n]) < horizon and n < read[reader] + fillers[items[n][0]][1] and all(d in done for d in needs(items[n])):
+                    ahead.append(items[n])
+                    n = n + 1
+                filled[reader] = n
+            for item in sorted(ahead, key=steps.index):
+                banks[item] = fillers[item[0]][0](*item[1:])
+            if step[0] in fillers:
+                step[0](banks[step], *step[1:])
+                reader = "vector" if step[0] in (product, mask) else "scalar"
+                read[reader] = read[reader] + 1
+            else:
+                step[0](*step[1:])
+            done.add(step)
+            if step[0] == quantize_features:
+                for j in range(step[3], step[3] + step[4]):
+                    done.add((step[1], 2 * step[2] + j))

@@ -18,17 +18,22 @@ ACT = mybir.ActivationFunctionType
 
 P = 128
 PACK = 4
+RUN = 8
 GROUP = 256
-GROUPS = S // GROUP
-BANK = 512
-SB = 5
-LS = 3
-LV = 3
 HALF = 512
-ROW_TILES = S // P
-Z_SCALE = 2.0 ** -10
-PARTS = 3
+BANK = 512
+GROUPS = S // GROUP
+TILES = S // P
+
+Z_SCALE = 2.0**-10
+OUT_SCALE = 1024.0
 EXTRA = 8
+ROOT_OF_EXTRA = 16.0
+PARTS = 3
+
+SCALAR_BANKS = 5
+VECTOR_BANKS = 3
+AHEAD = 3
 
 
 def tile_polysketchdegreefourcausalweights_w8_kernel(
@@ -37,39 +42,40 @@ def tile_polysketchdegreefourcausalweights_w8_kernel(
     nc = tc.nc
     with ExitStack() as ctx:
         keep = ctx.enter_context(tc.tile_pool(name="keep", bufs=1))
-        work = ctx.enter_context(tc.tile_pool(name="work", bufs=3))
-        psum = ctx.enter_context(tc.psum_pool(name="psum", bufs=2))
+        psum = ctx.enter_context(tc.psum_pool(name="psum", bufs=1))
         ctx.enter_context(tc.manual_schedule())
 
         def kept(name, shape, dtype):
             return keep.tile(shape, dtype, name=name, align_bytes=64)
 
         def scalar_bank(shape):
-            return psum.tile(shape, F32, name="scalar_bank", bufs=SB)
+            return psum.tile(shape, F32, name="scalar_bank", bufs=SCALAR_BANKS)
 
         def vector_bank(shape):
-            return psum.tile(shape, F32, name="vector_bank", bufs=8 - SB)
+            return psum.tile(shape, F32, name="vector_bank", bufs=VECTOR_BANKS)
 
         ident = kept("ident", [P, P], F32)
         pick = kept("pick", [P, 2 * PACK], BF16)
         factor_rows = kept("factor_rows", [P, P], BF16)
         factors = kept("factors", [P, 2 * PACK], F32)
+        factor_col = {"k": 0, "q": PACK}
         scale_cols = kept("scale_cols", [P, PACK], F32)
         scale_rows = kept("scale_rows", [P, D], F32)
         causal = kept("causal", [P, 2 * P], F32)
         zeros = kept("zeros", [P, 2 * P], F32)
-        sums = kept("sums", [P, ROW_TILES, PARTS], F32)
-        w_raw = [kept("w_raw%d" % g, [P, R], U32) for g in range(2)]
-        w_codes = [kept("w_codes%d" % g, [P, R], U32) for g in range(2)]
-        ws_raw = [kept("ws_raw%d" % g, [P, R], U8) for g in range(2)]
-        w_scales = [kept("w_scales%d" % g, [P, R], U8) for g in range(2)]
-        k_rows = [kept("k_rows%d" % g, [P, 2 * D], BF16) for g in range(2)]
+        sums = kept("sums", [P, TILES, PARTS], F32)
+        w_raw = [kept("w_raw%d" % w, [P, R], U32) for w in range(2)]
+        w_codes = [kept("w_codes%d" % w, [P, R], U32) for w in range(2)]
+        ws_raw = [kept("ws_raw%d" % w, [P, R], U8) for w in range(2)]
+        w_scales = [kept("w_scales%d" % w, [P, R], U8) for w in range(2)]
+        k_early = [kept("k_early%d" % g, [P, 2 * D], BF16) for g in range(2)]
         k_late = kept("k_late", [P, 4 * D], BF16)
-        k_rows = [k_rows[0][:], k_rows[1][:], k_late[:, : 2 * D], k_late[:, 2 * D :]]
         q_halves = [kept("qbytes%d" % h, [P, 4 * D], U8) for h in range(2)]
-        q_raw = [q_halves[g // 2][:, 2 * D * (g % 2) : 2 * D * (g % 2 + 1)] for g in range(GROUPS)]
         q_rows = [kept("q_rows%d" % g, [P, 2 * D], BF16) for g in range(GROUPS)]
-        rows = {"k": k_rows, "q": q_rows}
+        rows = {
+            "k": [k_early[0][:], k_early[1][:], k_late[:, : 2 * D], k_late[:, 2 * D :]],
+            "q": [tile[:] for tile in q_rows],
+        }
         turned = {(x, h): kept("turned_%s%d" % (x, h), [P, HALF * PACK], BF16) for x in "kq" for h in range(2)}
         first = {(x, h): kept("first_%s%d" % (x, h), [P, PACK, HALF], F32) for x in "kq" for h in range(2)}
         features = {(x, g): kept("features_%s%d" % (x, g), [P, GROUP * PACK], BF16) for x in "kq" for g in range(GROUPS)}
@@ -77,25 +83,13 @@ def tile_polysketchdegreefourcausalweights_w8_kernel(
         x_scales = {x: kept("x_scales_" + x, [P, S], U8) for x in "kq"}
         f_codes = {x: kept("f_codes_" + x, [P, S], U32) for x in "kq"}
         f_scales = {x: kept("f_scales_" + x, [P, S], U8) for x in "kq"}
-        weights = [kept("weights%d" % i, [P, P * (i + 1) + EXTRA], F32) for i in range(ROW_TILES)]
-        factor_col = {"k": 0, "q": PACK}
-        live = {}
-        sixteens = kept("sixteens", [P, ROW_TILES, EXTRA], F32)
-        masked = kept("masked", [P, ROW_TILES, P + EXTRA], F32)
-        den = kept("den", [P, ROW_TILES], F32)
-        inv = kept("inv", [P, ROW_TILES], F32)
+        weights = [kept("weights%d" % i, [P, P * (i + 1) + EXTRA], F32) for i in range(TILES)]
+        roots = kept("roots", [P, TILES, EXTRA], F32)
+        masked = kept("masked", [P, TILES, P + EXTRA], F32)
+        den = kept("den", [P, TILES], F32)
+        inv = kept("inv", [P, TILES], F32)
+        inv_scaled = kept("inv_scaled", [P, TILES], F32)
 
-        def warm_up():
-            bank = vector_bank([P, 2 * P])
-            nc.tensor.matmul(bank[:], lhsT=zeros[:, :P], rhs=zeros[:], start=True, stop=True)
-
-        def load_weight_scales(g, src, *which):
-            src_rows = src[0].bitcast(I32)
-            for r in which:
-                nc.sync.dma_start(out=ws_raw[g][r:P:32, :].bitcast(I32), in_=src_rows[r:16:4, :])
-
-        def load_weight_words(g, src):
-            nc.sync.dma_start(out=w_raw[g][:].bitcast(I32), in_=src[0].rearrange("p n t -> p (n t)").bitcast(I32))
 
         def load_rows(dst, src, g0, count):
             nc.sync.dma_start(
@@ -103,24 +97,32 @@ def tile_polysketchdegreefourcausalweights_w8_kernel(
                 in_=src[0, GROUP * g0 : GROUP * (g0 + count), :].rearrange("(g p j) d -> p g (j d)", j=2, p=P),
             )
 
+        def load_weight_words(w, src):
+            nc.sync.dma_start(out=w_raw[w][:].bitcast(I32), in_=src[0].rearrange("p n t -> p (n t)").bitcast(I32))
+
+        def load_weight_scales(w, src):
+            src_rows = src[0].bitcast(I32)
+            for r in range(4):
+                nc.sync.dma_start(out=ws_raw[w][r:P:32, :].bitcast(I32), in_=src_rows[r:16:4, :])
+
         def load_factor(x, src):
             c = factor_col[x]
             nc.sync.dma_start(
-                out=factor_rows[c : c + PACK, :].rearrange("t (b j) -> t b j", j=8),
-                in_=src.rearrange("(b t j) -> t b j", t=PACK, j=8),
+                out=factor_rows[c : c + PACK, :].rearrange("t (n j) -> t n j", j=RUN),
+                in_=src.rearrange("(n t j) -> t n j", t=PACK, j=RUN),
             )
 
-        def order_words(g):
-            nc.vector.tensor_copy(
-                out=w_codes[g][:].bitcast(I32).rearrange("p (t b j) -> p t b j", t=PACK, j=8),
-                in_=w_raw[g][:].bitcast(I32).rearrange("p (b t j) -> p t b j", t=PACK, j=8),
-            )
 
-        def order_scales(g):
-            nc.vector.tensor_copy(
-                out=w_scales[g][:].bitcast(I32).rearrange("p (t b j) -> p t b j", t=PACK, j=2),
-                in_=ws_raw[g][:].bitcast(I32).rearrange("p (b t j) -> p t b j", t=PACK, j=2),
-            )
+        def warm_up():
+            bank = vector_bank([P, 2 * P])
+            nc.tensor.matmul(bank[:], lhsT=zeros[:, :P], rhs=zeros[:], start=True, stop=True)
+
+        def order_weight(w):
+            for dst, src, run in ((w_codes, w_raw, RUN), (w_scales, ws_raw, RUN // 4)):
+                nc.vector.tensor_copy(
+                    out=dst[w][:].bitcast(I32).rearrange("p (t n j) -> p t n j", t=PACK, j=run),
+                    in_=src[w][:].bitcast(I32).rearrange("p (n t j) -> p t n j", t=PACK, j=run),
+                )
 
         def spread_scale_in():
             bank = scalar_bank([P, PACK, P])
@@ -140,15 +142,20 @@ def tile_polysketchdegreefourcausalweights_w8_kernel(
             nc.scalar.copy(out=factors[:], in_=bank[:])
 
         def widen(g, j):
-            cols = slice(D * j, D * (j + 1))
-            nc.vector.tensor_tensor(out=q_rows[g][:, cols], in0=q_raw[g][:, cols].bitcast(FP8), in1=scale_rows[:], op=ALU.mult)
+            c0 = 2 * D * (g % 2) + D * j
+            nc.vector.tensor_tensor(
+                out=q_rows[g][:, D * j : D * (j + 1)],
+                in0=q_halves[g // 2][:, c0 : c0 + D].bitcast(FP8),
+                in1=scale_rows[:],
+                op=ALU.mult,
+            )
 
         def turn_in(x, g):
-            words = rows[x][g][:].bitcast(F32)
+            words = rows[x][g].bitcast(F32)
             bank = scalar_bank([P, 2, 2, P])
             for j in range(2):
                 for u in range(2):
-                    nc.tensor.transpose(bank[:, j, u, :], words[:, 256 * j + u : 256 * (j + 1) : 2], ident[:])
+                    nc.tensor.transpose(bank[:, j, u, :], words[:, D // 2 * j + u : D // 2 * (j + 1) : 2], ident[:])
             return bank
 
         def turn(bank, x, g):
@@ -165,16 +172,16 @@ def tile_polysketchdegreefourcausalweights_w8_kernel(
         def quantize_rows(x, h):
             quantize(turned[x, h][:], x_codes[x], x_scales[x], HALF * h)
 
-        def quantize_features(x, g, j0=0, count=2):
-            src = features[x, g][:, PACK * P * j0 : PACK * P * (j0 + count)]
-            quantize(src, f_codes[x], f_scales[x], GROUP * g + P * j0)
+        def quantize_features(x, i0, count):
+            j0 = i0 % 2
+            quantize(features[x, i0 // 2][:, PACK * P * j0 : PACK * P * (j0 + count)], f_codes[x], f_scales[x], P * i0)
 
-        def project(dst, g, t, x, cols):
+        def project(dst, w, t, x, cols):
             w_cols = slice(P * t, P * (t + 1))
             nc.tensor.matmul_mx(
                 dst,
-                lhsT=w_codes[g][:, w_cols].bitcast(FP8X4),
-                lhsT_scale=w_scales[g][:, w_cols],
+                lhsT=w_codes[w][:, w_cols].bitcast(FP8X4),
+                lhsT_scale=w_scales[w][:, w_cols],
                 rhs=x_codes[x][:, cols].bitcast(FP8X4),
                 rhs_scale=x_scales[x][:, cols],
                 start=True,
@@ -190,18 +197,19 @@ def tile_polysketchdegreefourcausalweights_w8_kernel(
             c = factor_col[x] + t
             nc.scalar.activation(out=first[x, h][:, t, :], in_=bank[:], func=ACT.Copy, scale=factors[:, c : c + 1])
 
-        def product_in(x, g, j):
+        def product_in(x, i):
             bank = vector_bank([P, PACK, P])
             for t in range(PACK):
-                project(bank[:, t, :], 1, t, x, slice(GROUP * g + P * j, GROUP * g + P * (j + 1)))
+                project(bank[:, t, :], 1, t, x, slice(P * i, P * (i + 1)))
             return bank
 
-        def product(bank, x, g, j):
-            c0 = GROUP * (g % 2) + P * j
+        def product(bank, x, i):
+            c0 = P * (i % 4)
+            dst = features[x, i // 2][:, PACK * P * (i % 2) : PACK * P * (i % 2 + 1)]
             nc.vector.tensor_tensor(
-                out=features[x, g][:, PACK * P * j : PACK * P * (j + 1)].rearrange("p (c i t) -> p c t i", i=4, t=PACK),
-                in0=bank[:].rearrange("p t (c i) -> p c t i", i=4),
-                in1=first[x, g // 2][:, :, c0 : c0 + P].rearrange("p t (c i) -> p c t i", i=4),
+                out=dst.rearrange("p (c n t) -> p c t n", n=4, t=PACK),
+                in0=bank[:].rearrange("p t (c n) -> p c t n", n=4),
+                in1=first[x, i // 4][:, :, c0 : c0 + P].rearrange("p t (c n) -> p c t n", n=4),
                 op=ALU.mult,
             )
 
@@ -239,11 +247,11 @@ def tile_polysketchdegreefourcausalweights_w8_kernel(
         def square_past_in(i, c0):
             width = min(BANK, P * i - c0)
             bank = scalar_bank([P, width])
-            done = 0
+            covered = 0
             for n in (512, 256, 128):
-                if width - done >= n:
-                    scores(bank[:, done : done + n], i, c0 + done, n)
-                    done = done + n
+                if width - covered >= n:
+                    scores(bank[:, covered : covered + n], i, c0 + covered, n)
+                    covered = covered + n
             return bank
 
         def square_past(bank, i, c0):
@@ -257,229 +265,180 @@ def tile_polysketchdegreefourcausalweights_w8_kernel(
             )
 
         def row_sums(i0, count):
-            nc.vector.tensor_reduce(out=den[:, i0 : i0 + count], in_=sums[:, i0 : i0 + count, :], axis=mybir.AxisListType.X, op=ALU.add)
+            nc.vector.tensor_reduce(
+                out=den[:, i0 : i0 + count], in_=sums[:, i0 : i0 + count, :], axis=mybir.AxisListType.X, op=ALU.add
+            )
 
         def invert(i0, count):
-            src = sums[:, 0, 0:1] if i0 + count == 1 else den[:, i0 : i0 + count]
+            src = sums[:, 0, 0:1] if i0 == 0 else den[:, i0 : i0 + count]
             nc.vector.reciprocal(out=inv[:, i0 : i0 + count], in_=src)
 
-        def normalise(i, engine="V"):
-            col = inv[:, i : i + 1]
+        def divide_on_vector(i):
             row = weights[i][:, : P * (i + 1)]
-            if engine == "S":
-                factor = work.tile([P, 1], F32, name="factor")
-                nc.scalar.activation(out=factor[:], in_=col, func=ACT.Copy, scale=1024.0)
-                nc.scalar.activation(out=row, in_=row, func=ACT.Copy, scale=factor[:])
-            else:
-                eng = nc.vector if engine == "V" else nc.gpsimd
-                eng.tensor_scalar(out=row, in0=row, scalar1=col, scalar2=1024.0, op0=ALU.mult, op1=ALU.mult)
+            nc.vector.tensor_scalar(
+                out=row, in0=row, scalar1=inv[:, i : i + 1], scalar2=OUT_SCALE, op0=ALU.mult, op1=ALU.mult
+            )
+
+        def scale_inverse(i):
+            nc.scalar.activation(out=inv_scaled[:, i : i + 1], in_=inv[:, i : i + 1], func=ACT.Copy, scale=OUT_SCALE)
+
+        def divide_on_scalar(i):
+            row = weights[i][:, : P * (i + 1)]
+            nc.scalar.activation(out=row, in_=row, func=ACT.Copy, scale=inv_scaled[:, i : i + 1])
 
         def store(i):
             nc.sync.dma_start(out=out[0, P * i : P * (i + 1), : P * (i + 1)], in_=weights[i][:, : P * (i + 1)])
 
         nc.vector.memset(zeros[:], 0.0)
-        for g in range(2):
-            nc.vector.memset(ws_raw[g][:].bitcast(I32), 0)
+        for w in range(2):
+            nc.vector.memset(ws_raw[w][:].bitcast(I32), 0)
         nc.vector.memset(ident[:], 0.0)
         make_identity(nc, ident[:], nomemset=True)
         nc.vector.memset(factor_rows[:].bitcast(I32), 0)
-        nc.vector.memset(sixteens[:], 16.0)
+        nc.vector.memset(roots[:], ROOT_OF_EXTRA)
         nc.vector.memset(sums[:], 0.0)
         nc.vector.memset(causal[:], 1.0)
-        nc.scalar.activation(out=masked[:, :, P:], in_=sixteens[:], func=ACT.Square)
+        nc.scalar.activation(out=masked[:, :, P:], in_=roots[:], func=ACT.Square)
         nc.gpsimd.affine_select(
             out=causal[:], in_=causal[:], pattern=[[0, 2], [-1, P]], compare_op=ALU.is_ge, fill=0.0, base=0, channel_multiplier=1
         )
         nc.vector.tensor_copy(out=pick[:], in_=ident[:, : 2 * PACK])
 
         nc.sync.dma_start(out=scale_cols[:], in_=q_scale[0, 0].rearrange("(p t) -> p t", t=PACK))
-        load_rows(k_rows[0], k, 0, 1)
-        load_rows(k_rows[1], k, 1, 1)
+        load_rows(k_early[0][:], k, 0, 1)
         load_rows(q_halves[1][:], q_bytes, 2, 2)
+        load_rows(k_early[1][:], k, 1, 1)
         load_weight_words(0, g1_words)
-        load_weight_scales(0, g1_scales, 0, 1, 2, 3)
+        load_weight_scales(0, g1_scales)
         load_factor("k", b)
         load_factor("q", a)
         load_weight_words(1, g2_words)
-        load_weight_scales(1, g2_scales, 0, 1, 2, 3)
+        load_weight_scales(1, g2_scales)
         load_rows(q_halves[0][:], q_bytes, 0, 2)
         load_rows(k_late[:], k, 2, 2)
-        for i in range(ROW_TILES - 1):
-            blocks = ROW_TILES - 1 - i
+        for i in range(TILES - 1):
             nc.sync.dma_start(
                 out=out[0, P * i : P * (i + 1), P * (i + 1) :].rearrange("p (n c) -> p n c", c=P),
-                in_=zeros[:, :P].unsqueeze(1).to_broadcast([P, blocks, P]),
+                in_=zeros[:, :P].unsqueeze(1).to_broadcast([P, TILES - 1 - i, P]),
             )
-        steps = [
-            (warm_up,),
-            (spread_scale,),
-            (warm_up,),
-            (turn, "k", 0),
-            (turn, "k", 1),
-            (warm_up,),
-            (widen, 2, 0),
-            (widen, 2, 1),
-            (order_words, 0),
-            (order_scales, 0),
-            (turn, "q", 2),
-            (turn_factors,),
-            (warm_up,),
-            (quantize_rows, "k", 0),
-            (first_projection, "k", 0, 0),
-            (first_projection, "k", 0, 1),
-            (widen, 3, 0),
-            (widen, 3, 1),
-            (turn, "q", 3),
-            (first_projection, "k", 0, 2),
-            (order_words, 1),
-            (order_scales, 1),
-            (widen, 1, 0),
-            (first_projection, "k", 0, 3),
-            (widen, 1, 1),
-            (widen, 0, 0),
-            (quantize_rows, "q", 1),
-            (turn, "k", 2),
-            (turn, "k", 3),
-            (first_projection, "q", 1, 0),
-            (first_projection, "q", 1, 1),
-            (widen, 0, 1),
-            (product, "k", 0, 0),
-            (product, "k", 0, 1),
-            (turn, "q", 1),
-            (first_projection, "q", 1, 2),
-            (first_projection, "q", 1, 3),
-            (quantize_rows, "k", 1),
-            (quantize_features, "k", 0, 0, 2),
-            (turn, "q", 0),
-            (product, "k", 1, 0),
-            (first_projection, "k", 1, 0),
-            (first_projection, "k", 1, 1),
-            (product, "k", 1, 1),
-            (product, "q", 2, 0),
-            (first_projection, "k", 1, 2),
-            (quantize_rows, "q", 0),
-            (product, "q", 2, 1),
-            (first_projection, "k", 1, 3),
-            (quantize_features, "k", 1, 0, 2),
-            (quantize_features, "q", 2, 0, 2),
-            (first_projection, "q", 0, 0),
-            (first_projection, "q", 0, 1),
-            (product, "q", 3, 0),
-            (first_projection, "q", 0, 2),
-            (product, "q", 3, 1),
-            (first_projection, "q", 0, 3),
-            (square_past, 5, 0),
-            (product, "k", 2, 0),
-            (square_past, 4, 0),
-            (quantize_features, "q", 3, 0, 2),
-            (product, "k", 2, 1),
-            (square_past, 7, 0),
-            (product, "k", 3, 0),
-            (quantize_features, "k", 2, 0, 2),
-            (square_past, 5, BANK),
-            (product, "k", 3, 1),
-            (mask, 4, 2),
-            (square_diagonal, 5),
-            (square_diagonal, 4),
-            (square_past, 6, 0),
-            (quantize_features, "k", 3, 0, 2),
-            (square_past, 6, BANK),
-            (product, "q", 1, 0),
-            (square_past, 7, BANK),
-            (row_sums, 4, 2),
-            (mask, 6, 2),
-            (invert, 4, 2),
-            (square_diagonal, 7),
-            (square_diagonal, 6),
-            (product, "q", 1, 1),
-            (normalise, 5, "V"),
-            (store, 5),
-            (quantize_features, "q", 1, 0, 2),
-            (square_past, 3, 0),
-            (square_past, 2, 0),
-            (row_sums, 6, 2),
-            (normalise, 4, "V"),
-            (store, 4),
-            (invert, 6, 2),
-            (product, "q", 0, 1),
-            (mask, 2, 2),
-            (square_diagonal, 3),
-            (square_diagonal, 2),
-            (normalise, 7, "V"),
-            (store, 7),
-            (normalise, 6, "S"),
-            (product, "q", 0, 0),
-            (quantize_features, "q", 0, 1, 1),
-            (row_sums, 2, 2),
-            (quantize_features, "q", 0, 0, 1),
-            (store, 6),
-            (square_past, 1, 0),
-            (invert, 2, 2),
-            (mask, 1, 1),
-            (square_diagonal, 1),
-            (mask, 0, 1),
-            (square_diagonal, 0),
-            (normalise, 3, "V"),
-            (store, 3),
-            (row_sums, 1, 1),
-            (normalise, 2, "V"),
-            (store, 2),
-            (invert, 1, 1),
-            (invert, 0, 1),
-            (normalise, 1, "V"),
-            (store, 1),
-            (normalise, 0, "V"),
-            (store, 0),
-        ]
+
+        halves = [("k", 0), ("q", 1), ("k", 1), ("q", 0)]
+
+        on_scalar = [(spread_scale,), (turn, "k", 0), (turn, "k", 1), (turn, "q", 2), (turn_factors,)]
+        turns_after = [[("q", 3)], [("k", 2), ("k", 3)], [("q", 1)], [("q", 0)], [], [], [], []]
+        for n, groups in enumerate(turns_after):
+            on_scalar += [(first_projection,) + halves[n // 2] + (2 * (n % 2) + e,) for e in range(2)]
+            on_scalar += [(turn,) + group for group in groups]
+        on_scalar += [(square_past, i, 0) for i in (5, 4, 7, 6)]
+        on_scalar += [(square_past, 5, BANK), (square_diagonal, 5), (square_diagonal, 4), (square_past, 6, BANK)]
+        on_scalar += [(square_past, 7, BANK), (square_diagonal, 6), (scale_inverse, 5), (square_diagonal, 7)]
+        on_scalar += [(divide_on_scalar, 5), (square_past, 3, 0), (square_past, 2, 0), (square_diagonal, 3)]
+        on_scalar += [(scale_inverse, 6), (square_diagonal, 2), (divide_on_scalar, 6), (store, 6)]
+        on_scalar += [(square_past, 1, 0), (square_diagonal, 1), (square_diagonal, 0)]
+
+        on_vector = [(widen, 2, 0), (widen, 2, 1), (order_weight, 0), (quantize_rows, "k", 0)]
+        on_vector += [(widen, 3, 0), (widen, 3, 1), (order_weight, 1)]
+        on_vector += [(widen, 1, 0), (widen, 1, 1), (widen, 0, 0), (quantize_rows, "q", 1), (widen, 0, 1)]
+        tiles = [(x, 4 * h + j) for x, h in halves[:3] for j in range(4)]
+        rows_after = {1: halves[2], 4: halves[3]}
+        for n, (x, i) in enumerate(tiles):
+            on_vector += [(product, x, i)]
+            if n in rows_after:
+                on_vector += [(quantize_rows,) + rows_after[n]]
+            if n > 0 and n % 2 == 0:
+                on_vector += [(quantize_features,) + tiles[n - 2] + (2,)]
+        on_vector += [(mask, 4, 2), (quantize_features, "k", 6, 2), (product, "q", 2), (row_sums, 4, 2), (mask, 6, 2)]
+        on_vector += [(invert, 4, 2), (product, "q", 3), (divide_on_vector, 4), (store, 4)]
+        on_vector += [(quantize_features, "q", 2, 2), (row_sums, 6, 2), (product, "q", 1), (invert, 6, 2), (store, 5)]
+        on_vector += [(mask, 2, 2), (divide_on_vector, 7), (store, 7), (product, "q", 0)]
+        on_vector += [(quantize_features, "q", 1, 1), (row_sums, 2, 2), (quantize_features, "q", 0, 1), (invert, 2, 2)]
+        on_vector += [(mask, 1, 1), (mask, 0, 1), (divide_on_vector, 3), (store, 3), (row_sums, 1, 1)]
+        on_vector += [(divide_on_vector, 2), (store, 2), (invert, 1, 1), (invert, 0, 1)]
+        on_vector += [(divide_on_vector, 1), (store, 1), (divide_on_vector, 0), (store, 0)]
+
         fillers = {
-            spread_scale: (spread_scale_in, LS),
-            turn_factors: (turn_factors_in, LS),
-            turn: (turn_in, LS),
-            first_projection: (first_projection_in, LS),
-            square_past: (square_past_in, LS),
-            product: (product_in, LV),
-            mask: (mask_in, LV),
+            spread_scale: spread_scale_in,
+            turn_factors: turn_factors_in,
+            turn: turn_in,
+            first_projection: first_projection_in,
+            square_past: square_past_in,
+            product: product_in,
+            mask: mask_in,
         }
+
+        def bank_needs(step):
+            f, args = step[0], step[1:]
+            if f == turn and args[0] == "q":
+                return [(widen, args[1], 1)]
+            if f == turn and args[1] >= 2:
+                return [(order_weight, 1)]
+            if f == first_projection:
+                return [(quantize_rows, args[0], args[1]), (order_weight, 0)]
+            if f == product:
+                return [(quantize_rows, args[0], args[1] // 4), (order_weight, 1)]
+            if f == square_past:
+                return [("codes", "q", args[0]), ("codes", "k", min(args[0], (args[1] + BANK) // P) - 1)]
+            if f == mask:
+                return [("codes", x, i) for x in "qk" for i in range(args[0], args[0] + args[1])]
+            return []
 
         def needs(step):
             f, args = step[0], step[1:]
-            if f == turn and args[0] == "q":
-                return [(widen, args[1], 0), (widen, args[1], 1)]
-            if f == first_projection:
-                return [(quantize_rows, args[0], args[1]), (order_scales, 0)]
+            if f == widen:
+                return [(spread_scale,)]
+            if f == quantize_rows:
+                return [(turn, args[0], 2 * args[1]), (turn, args[0], 2 * args[1] + 1)]
             if f == product:
-                return [(quantize_rows, args[0], args[1] // 2), (order_scales, 1)]
-            if f == square_past:
-                last_tile = min(args[0], (args[1] + BANK) // P) - 1
-                return [("q", args[0]), ("k", last_tile)]
-            if f == mask:
-                return [(x, i) for x in "qk" for i in range(args[0], args[0] + args[1])]
-            return []
+                return [(first_projection, args[0], args[1] // 4, PACK - 1)]
+            if f == square_diagonal:
+                return [("masked", args[0])]
+            if f in (row_sums, invert):
+                return [(square_diagonal, i) for i in range(args[0], args[0] + args[1])]
+            if f == scale_inverse:
+                return [("inverse", args[0])]
+            if f == store:
+                return [("divided", args[0])]
+            return bank_needs(step)
 
-        done = set()
+        def makes(step):
+            f, args = step[0], step[1:]
+            if f == quantize_features:
+                return [("codes", args[0], i) for i in range(args[1], args[1] + args[2])]
+            if f == mask:
+                return [("masked", i) for i in range(args[0], args[0] + args[1])]
+            if f == invert:
+                return [("inverse", i) for i in range(args[0], args[0] + args[1])]
+            if f in (divide_on_vector, divide_on_scalar):
+                return [("divided", args[0])]
+            return [step]
+
+        programs = [on_vector, on_scalar]
+        with_bank = [[step for step in program if step[0] in fillers] for program in programs]
+        warm_before = [(spread_scale,), (turn, "k", 0), (turn, "q", 2), (first_projection, "k", 0, 0)]
+        written = []
         banks = {}
-        streams = {reader: [s for s in steps if s[0] in fillers and (s[0] in (product, mask)) == (reader == "vector")] for reader in ("scalar", "vector")}
-        read = {"scalar": 0, "vector": 0}
-        filled = {"scalar": 0, "vector": 0}
-        for at, step in enumerate(steps):
-            horizon = min([n for n in range(at, len(steps)) if steps[n] == (warm_up,)] + [len(steps)])
-            ahead = []
-            for reader in streams:
-                items = streams[reader]
-                n = filled[reader]
-                while n < len(items) and steps.index(items[n]) < horizon and n < read[reader] + fillers[items[n][0]][1] and all(d in done for d in needs(items[n])):
-                    ahead.append(items[n])
-                    n = n + 1
-                filled[reader] = n
-            for item in sorted(ahead, key=steps.index):
-                banks[item] = fillers[item[0]][0](*item[1:])
-            if step[0] in fillers:
-                step[0](banks[step], *step[1:])
-                reader = "vector" if step[0] in (product, mask) else "scalar"
-                read[reader] = read[reader] + 1
-            else:
-                step[0](*step[1:])
-            done.add(step)
-            if step[0] == quantize_features:
-                for j in range(step[3], step[3] + step[4]):
-                    done.add((step[1], 2 * step[2] + j))
+        at, read, filled = [0, 0], [0, 0], [0, 0]
+
+        def fill_ahead(e):
+            for step in with_bank[e][filled[e] : read[e] + AHEAD]:
+                if not all(need in written for need in bank_needs(step)):
+                    return
+                if step in warm_before:
+                    warm_up()
+                banks[step] = fillers[step[0]](*step[1:])
+                filled[e] = filled[e] + 1
+
+        for visit in range(2 * (len(on_vector) + len(on_scalar))):
+            e = visit % 2
+            if at[e] < len(programs[e]) and all(need in written for need in needs(programs[e][at[e]])):
+                step = programs[e][at[e]]
+                at[e] = at[e] + 1
+                fill_ahead(0)
+                fill_ahead(1)
+                if step[0] in fillers:
+                    step[0](banks[step], *step[1:])
+                    read[e] = read[e] + 1
+                else:
+                    step[0](*step[1:])
+                written.extend(makes(step))
+        assert at == [len(on_vector), len(on_scalar)]

from contextlib import ExitStack

import concourse.mybir as mybir
from concourse.masks import make_identity

S, D, R = 1024, 512, 512
FLOPS = 4 * 2 * S * D * R + 2 * S * S * R

F32 = mybir.dt.float32
BF16 = mybir.dt.bfloat16
I32 = mybir.dt.int32
U32 = mybir.dt.uint32
U8 = mybir.dt.uint8
FP8 = mybir.dt.float8_e4m3fn
FP8X4 = mybir.dt.float8_e4m3fn_x4
ALU = mybir.AluOpType
ACT = mybir.ActivationFunctionType

P = 128
PACK = 4
RUN = 8
GROUP = 256
HALF = 512
BANK = 512
GROUPS = S // GROUP
TILES = S // P

Z_SCALE = 2.0**-10
OUT_SCALE = 1024.0
EXTRA = 8
ROOT_OF_EXTRA = 16.0
PARTS = 3

SCALAR_BANKS = 5
VECTOR_BANKS = 3
AHEAD = 3


def tile_polysketchdegreefourcausalweights_w8_kernel(
    tc, q_bytes, q_scale, k, g1_words, g1_scales, g2_words, g2_scales, a, b, out
):
    nc = tc.nc
    with ExitStack() as ctx:
        keep = ctx.enter_context(tc.tile_pool(name="keep", bufs=1))
        psum = ctx.enter_context(tc.psum_pool(name="psum", bufs=1))
        ctx.enter_context(tc.manual_schedule())

        def kept(name, shape, dtype):
            return keep.tile(shape, dtype, name=name, align_bytes=64)

        def scalar_bank(shape):
            return psum.tile(shape, F32, name="scalar_bank", bufs=SCALAR_BANKS)

        def vector_bank(shape):
            return psum.tile(shape, F32, name="vector_bank", bufs=VECTOR_BANKS)

        ident = kept("ident", [P, P], F32)
        pick = kept("pick", [P, 2 * PACK], BF16)
        factor_rows = kept("factor_rows", [P, P], BF16)
        factors = kept("factors", [P, 2 * PACK], F32)
        factor_col = {"k": 0, "q": PACK}
        scale_cols = kept("scale_cols", [P, PACK], F32)
        scale_rows = kept("scale_rows", [P, D], F32)
        causal = kept("causal", [P, 2 * P], F32)
        zeros = kept("zeros", [P, 2 * P], F32)
        sums = kept("sums", [P, TILES, PARTS], F32)
        w_raw = [kept("w_raw%d" % w, [P, R], U32) for w in range(2)]
        w_codes = [kept("w_codes%d" % w, [P, R], U32) for w in range(2)]
        ws_raw = [kept("ws_raw%d" % w, [P, R], U8) for w in range(2)]
        w_scales = [kept("w_scales%d" % w, [P, R], U8) for w in range(2)]
        k_early = [kept("k_early%d" % g, [P, 2 * D], BF16) for g in range(2)]
        k_late = kept("k_late", [P, 4 * D], BF16)
        q_halves = [kept("qbytes%d" % h, [P, 4 * D], U8) for h in range(2)]
        q_rows = [kept("q_rows%d" % g, [P, 2 * D], BF16) for g in range(GROUPS)]
        rows = {
            "k": [k_early[0][:], k_early[1][:], k_late[:, : 2 * D], k_late[:, 2 * D :]],
            "q": [tile[:] for tile in q_rows],
        }
        turned = {(x, h): kept("turned_%s%d" % (x, h), [P, HALF * PACK], BF16) for x in "kq" for h in range(2)}
        first = {(x, h): kept("first_%s%d" % (x, h), [P, PACK, HALF], F32) for x in "kq" for h in range(2)}
        features = {(x, g): kept("features_%s%d" % (x, g), [P, GROUP * PACK], BF16) for x in "kq" for g in range(GROUPS)}
        x_codes = {x: kept("x_codes_" + x, [P, S], U32) for x in "kq"}
        x_scales = {x: kept("x_scales_" + x, [P, S], U8) for x in "kq"}
        f_codes = {x: kept("f_codes_" + x, [P, S], U32) for x in "kq"}
        f_scales = {x: kept("f_scales_" + x, [P, S], U8) for x in "kq"}
        weights = [kept("weights%d" % i, [P, P * (i + 1) + EXTRA], F32) for i in range(TILES)]
        roots = kept("roots", [P, TILES, EXTRA], F32)
        masked = kept("masked", [P, TILES, P + EXTRA], F32)
        den = kept("den", [P, TILES], F32)
        inv = kept("inv", [P, TILES], F32)
        inv_scaled = kept("inv_scaled", [P, TILES], F32)


        def load_rows(dst, src, g0, count):
            nc.sync.dma_start(
                out=dst.rearrange("p (g c) -> p g c", g=count),
                in_=src[0, GROUP * g0 : GROUP * (g0 + count), :].rearrange("(g p j) d -> p g (j d)", j=2, p=P),
            )

        def load_weight_words(w, src):
            nc.sync.dma_start(out=w_raw[w][:].bitcast(I32), in_=src[0].rearrange("p n t -> p (n t)").bitcast(I32))

        def load_weight_scales(w, src):
            src_rows = src[0].bitcast(I32)
            for r in range(4):
                nc.sync.dma_start(out=ws_raw[w][r:P:32, :].bitcast(I32), in_=src_rows[r:16:4, :])

        def load_factor(x, src):
            c = factor_col[x]
            nc.sync.dma_start(
                out=factor_rows[c : c + PACK, :].rearrange("t (n j) -> t n j", j=RUN),
                in_=src.rearrange("(n t j) -> t n j", t=PACK, j=RUN),
            )


        def warm_up():
            bank = vector_bank([P, 2 * P])
            nc.tensor.matmul(bank[:], lhsT=zeros[:, :P], rhs=zeros[:], start=True, stop=True)

        def order_weight(w):
            for dst, src, run in ((w_codes, w_raw, RUN), (w_scales, ws_raw, RUN // 4)):
                nc.vector.tensor_copy(
                    out=dst[w][:].bitcast(I32).rearrange("p (t n j) -> p t n j", t=PACK, j=run),
                    in_=src[w][:].bitcast(I32).rearrange("p (n t j) -> p t n j", t=PACK, j=run),
                )

        def spread_scale_in():
            bank = scalar_bank([P, PACK, P])
            for t in range(PACK):
                nc.tensor.transpose(bank[:, t, :], scale_cols[:, t : t + 1].to_broadcast([P, P]), ident[:])
            return bank

        def spread_scale(bank):
            nc.scalar.copy(out=scale_rows[:].rearrange("p (n t) -> p n t", t=PACK), in_=bank[:].rearrange("p t n -> p n t"))

        def turn_factors_in():
            bank = scalar_bank([P, 2 * PACK])
            nc.tensor.matmul(bank[:], lhsT=factor_rows[:], rhs=pick[:], start=True, stop=True)
            return bank

        def turn_factors(bank):
            nc.scalar.copy(out=factors[:], in_=bank[:])

        def widen(g, j):
            c0 = 2 * D * (g % 2) + D * j
            nc.vector.tensor_tensor(
                out=q_rows[g][:, D * j : D * (j + 1)],
                in0=q_halves[g // 2][:, c0 : c0 + D].bitcast(FP8),
                in1=scale_rows[:],
                op=ALU.mult,
            )

        def turn_in(x, g):
            words = rows[x][g].bitcast(F32)
            bank = scalar_bank([P, 2, 2, P])
            for j in range(2):
                for u in range(2):
                    nc.tensor.transpose(bank[:, j, u, :], words[:, D // 2 * j + u : D // 2 * (j + 1) : 2], ident[:])
            return bank

        def turn(bank, x, g):
            dst = turned[x, g // 2][:, GROUP * PACK * (g % 2) : GROUP * PACK * (g % 2 + 1)]
            nc.scalar.copy(
                out=dst.bitcast(F32).rearrange("p (r j u) -> p r j u", j=2, u=2),
                in_=bank[:].rearrange("p j u r -> p r j u"),
            )

        def quantize(src, codes, scales, c0):
            cols = slice(c0, c0 + src.shape[1] // PACK)
            nc.vector.quantize_mx(out=codes[:, cols].bitcast(FP8X4), scales=scales[:, cols], in_=src)

        def quantize_rows(x, h):
            quantize(turned[x, h][:], x_codes[x], x_scales[x], HALF * h)

        def quantize_features(x, i0, count):
            j0 = i0 % 2
            quantize(features[x, i0 // 2][:, PACK * P * j0 : PACK * P * (j0 + count)], f_codes[x], f_scales[x], P * i0)

        def project(dst, w, t, x, cols):
            w_cols = slice(P * t, P * (t + 1))
            nc.tensor.matmul_mx(
                dst,
                lhsT=w_codes[w][:, w_cols].bitcast(FP8X4),
                lhsT_scale=w_scales[w][:, w_cols],
                rhs=x_codes[x][:, cols].bitcast(FP8X4),
                rhs_scale=x_scales[x][:, cols],
                start=True,
                stop=True,
            )

        def first_projection_in(x, h, t):
            bank = scalar_bank([P, HALF])
            project(bank[:], 0, t, x, slice(HALF * h, HALF * (h + 1)))
            return bank

        def first_projection(bank, x, h, t):
            c = factor_col[x] + t
            nc.scalar.activation(out=first[x, h][:, t, :], in_=bank[:], func=ACT.Copy, scale=factors[:, c : c + 1])

        def product_in(x, i):
            bank = vector_bank([P, PACK, P])
            for t in range(PACK):
                project(bank[:, t, :], 1, t, x, slice(P * i, P * (i + 1)))
            return bank

        def product(bank, x, i):
            c0 = P * (i % 4)
            dst = features[x, i // 2][:, PACK * P * (i % 2) : PACK * P * (i % 2 + 1)]
            nc.vector.tensor_tensor(
                out=dst.rearrange("p (c n t) -> p c t n", n=4, t=PACK),
                in0=bank[:].rearrange("p t (c n) -> p c t n", n=4),
                in1=first[x, i // 4][:, :, c0 : c0 + P].rearrange("p t (c n) -> p c t n", n=4),
                op=ALU.mult,
            )

        def scores(dst, i, c0, width):
            q_cols = slice(P * i, P * (i + 1))
            nc.tensor.matmul_mx(
                dst,
                lhsT=f_codes["q"][:, q_cols].bitcast(FP8X4),
                lhsT_scale=f_scales["q"][:, q_cols],
                rhs=f_codes["k"][:, c0 : c0 + width].bitcast(FP8X4),
                rhs_scale=f_scales["k"][:, c0 : c0 + width],
                start=True,
                stop=True,
            )

        def mask_in(i0, count):
            bank = vector_bank([P, count, P])
            for j in range(count):
                scores(bank[:, j, :], i0 + j, P * (i0 + j), P)
            return bank

        def mask(bank, i0, count):
            nc.vector.tensor_tensor(
                out=masked[:, i0 : i0 + count, :P],
                in0=bank[:],
                in1=causal[:, : count * P].rearrange("p (j c) -> p j c", c=P),
                op=ALU.mult,
            )

        def square_diagonal(i):
            nc.scalar.activation(
                out=weights[i][:, P * i :], in_=masked[:, i, :], func=ACT.Square, scale=Z_SCALE, accum_out=sums[:, i, 0:1]
            )

        def square_past_in(i, c0):
            width = min(BANK, P * i - c0)
            bank = scalar_bank([P, width])
            covered = 0
            for n in (512, 256, 128):
                if width - covered >= n:
                    scores(bank[:, covered : covered + n], i, c0 + covered, n)
                    covered = covered + n
            return bank

        def square_past(bank, i, c0):
            part = 1 + c0 // BANK
            nc.scalar.activation(
                out=weights[i][:, c0 : c0 + bank.shape[1]],
                in_=bank[:],
                func=ACT.Square,
                scale=Z_SCALE,
                accum_out=sums[:, i, part : part + 1],
            )

        def row_sums(i0, count):
            nc.vector.tensor_reduce(
                out=den[:, i0 : i0 + count], in_=sums[:, i0 : i0 + count, :], axis=mybir.AxisListType.X, op=ALU.add
            )

        def invert(i0, count):
            src = sums[:, 0, 0:1] if i0 == 0 else den[:, i0 : i0 + count]
            nc.vector.reciprocal(out=inv[:, i0 : i0 + count], in_=src)

        def divide_on_vector(i):
            row = weights[i][:, : P * (i + 1)]
            nc.vector.tensor_scalar(
                out=row, in0=row, scalar1=inv[:, i : i + 1], scalar2=OUT_SCALE, op0=ALU.mult, op1=ALU.mult
            )

        def scale_inverse(i):
            nc.scalar.activation(out=inv_scaled[:, i : i + 1], in_=inv[:, i : i + 1], func=ACT.Copy, scale=OUT_SCALE)

        def divide_on_scalar(i):
            row = weights[i][:, : P * (i + 1)]
            nc.scalar.activation(out=row, in_=row, func=ACT.Copy, scale=inv_scaled[:, i : i + 1])

        def store(i):
            nc.sync.dma_start(out=out[0, P * i : P * (i + 1), : P * (i + 1)], in_=weights[i][:, : P * (i + 1)])

        nc.vector.memset(zeros[:], 0.0)
        for w in range(2):
            nc.vector.memset(ws_raw[w][:].bitcast(I32), 0)
        nc.vector.memset(ident[:], 0.0)
        make_identity(nc, ident[:], nomemset=True)
        nc.vector.memset(factor_rows[:].bitcast(I32), 0)
        nc.vector.memset(roots[:], ROOT_OF_EXTRA)
        nc.vector.memset(sums[:], 0.0)
        nc.vector.memset(causal[:], 1.0)
        nc.scalar.activation(out=masked[:, :, P:], in_=roots[:], func=ACT.Square)
        nc.gpsimd.affine_select(
            out=causal[:], in_=causal[:], pattern=[[0, 2], [-1, P]], compare_op=ALU.is_ge, fill=0.0, base=0, channel_multiplier=1
        )
        nc.vector.tensor_copy(out=pick[:], in_=ident[:, : 2 * PACK])

        nc.sync.dma_start(out=scale_cols[:], in_=q_scale[0, 0].rearrange("(p t) -> p t", t=PACK))
        load_rows(k_early[0][:], k, 0, 1)
        load_rows(q_halves[1][:], q_bytes, 2, 2)
        load_rows(k_early[1][:], k, 1, 1)
        load_weight_words(0, g1_words)
        load_weight_scales(0, g1_scales)
        load_factor("k", b)
        load_factor("q", a)
        load_weight_words(1, g2_words)
        load_weight_scales(1, g2_scales)
        load_rows(q_halves[0][:], q_bytes, 0, 2)
        load_rows(k_late[:], k, 2, 2)
        for i in range(TILES - 1):
            nc.sync.dma_start(
                out=out[0, P * i : P * (i + 1), P * (i + 1) :].rearrange("p (n c) -> p n c", c=P),
                in_=zeros[:, :P].unsqueeze(1).to_broadcast([P, TILES - 1 - i, P]),
            )

        halves = [("k", 0), ("q", 1), ("k", 1), ("q", 0)]

        on_scalar = [(spread_scale,), (turn, "k", 0), (turn, "k", 1), (turn, "q", 2), (turn_factors,)]
        turns_after = [[("q", 3)], [("k", 2), ("k", 3)], [("q", 1)], [("q", 0)], [], [], [], []]
        for n, groups in enumerate(turns_after):
            on_scalar += [(first_projection,) + halves[n // 2] + (2 * (n % 2) + e,) for e in range(2)]
            on_scalar += [(turn,) + group for group in groups]
        on_scalar += [(square_past, i, 0) for i in (5, 4, 7, 6)]
        on_scalar += [(square_past, 5, BANK), (square_diagonal, 5), (square_diagonal, 4), (square_past, 6, BANK)]
        on_scalar += [(square_past, 7, BANK), (square_diagonal, 6), (scale_inverse, 5), (square_diagonal, 7)]
        on_scalar += [(divide_on_scalar, 5), (square_past, 3, 0), (square_past, 2, 0), (square_diagonal, 3)]
        on_scalar += [(scale_inverse, 6), (square_diagonal, 2), (divide_on_scalar, 6), (store, 6)]
        on_scalar += [(square_past, 1, 0), (square_diagonal, 1), (square_diagonal, 0)]

        on_vector = [(widen, 2, 0), (widen, 2, 1), (order_weight, 0), (quantize_rows, "k", 0)]
        on_vector += [(widen, 3, 0), (widen, 3, 1), (order_weight, 1)]
        on_vector += [(widen, 1, 0), (widen, 1, 1), (widen, 0, 0), (quantize_rows, "q", 1), (widen, 0, 1)]
        tiles = [(x, 4 * h + j) for x, h in halves[:3] for j in range(4)]
        rows_after = {1: halves[2], 4: halves[3]}
        for n, (x, i) in enumerate(tiles):
            on_vector += [(product, x, i)]
            if n in rows_after:
                on_vector += [(quantize_rows,) + rows_after[n]]
            if n > 0 and n % 2 == 0:
                on_vector += [(quantize_features,) + tiles[n - 2] + (2,)]
        on_vector += [(mask, 4, 2), (quantize_features, "k", 6, 2), (product, "q", 2), (row_sums, 4, 2), (mask, 6, 2)]
        on_vector += [(invert, 4, 2), (product, "q", 3), (divide_on_vector, 4), (store, 4)]
        on_vector += [(quantize_features, "q", 2, 2), (row_sums, 6, 2), (product, "q", 1), (invert, 6, 2), (store, 5)]
        on_vector += [(mask, 2, 2), (divide_on_vector, 7), (store, 7), (product, "q", 0)]
        on_vector += [(quantize_features, "q", 1, 1), (row_sums, 2, 2), (quantize_features, "q", 0, 1), (invert, 2, 2)]
        on_vector += [(mask, 1, 1), (mask, 0, 1), (divide_on_vector, 3), (store, 3), (row_sums, 1, 1)]
        on_vector += [(divide_on_vector, 2), (store, 2), (invert, 1, 1), (invert, 0, 1)]
        on_vector += [(divide_on_vector, 1), (store, 1), (divide_on_vector, 0), (store, 0)]

        fillers = {
            spread_scale: spread_scale_in,
            turn_factors: turn_factors_in,
            turn: turn_in,
            first_projection: first_projection_in,
            square_past: square_past_in,
            product: product_in,
            mask: mask_in,
        }

        def bank_needs(step):
            f, args = step[0], step[1:]
            if f == turn and args[0] == "q":
                return [(widen, args[1], 1)]
            if f == turn and args[1] >= 2:
                return [(order_weight, 1)]
            if f == first_projection:
                return [(quantize_rows, args[0], args[1]), (order_weight, 0)]
            if f == product:
                return [(quantize_rows, args[0], args[1] // 4), (order_weight, 1)]
            if f == square_past:
                return [("codes", "q", args[0]), ("codes", "k", min(args[0], (args[1] + BANK) // P) - 1)]
            if f == mask:
                return [("codes", x, i) for x in "qk" for i in range(args[0], args[0] + args[1])]
            return []

        def needs(step):
            f, args = step[0], step[1:]
            if f == widen:
                return [(spread_scale,)]
            if f == quantize_rows:
                return [(turn, args[0], 2 * args[1]), (turn, args[0], 2 * args[1] + 1)]
            if f == product:
                return [(first_projection, args[0], args[1] // 4, PACK - 1)]
            if f == square_diagonal:
                return [("masked", args[0])]
            if f in (row_sums, invert):
                return [(square_diagonal, i) for i in range(args[0], args[0] + args[1])]
            if f == scale_inverse:
                return [("inverse", args[0])]
            if f == store:
                return [("divided", args[0])]
            return bank_needs(step)

        def makes(step):
            f, args = step[0], step[1:]
            if f == quantize_features:
                return [("codes", args[0], i) for i in range(args[1], args[1] + args[2])]
            if f == mask:
                return [("masked", i) for i in range(args[0], args[0] + args[1])]
            if f == invert:
                return [("inverse", i) for i in range(args[0], args[0] + args[1])]
            if f in (divide_on_vector, divide_on_scalar):
                return [("divided", args[0])]
            return [step]

        programs = [on_vector, on_scalar]
        with_bank = [[step for step in program if step[0] in fillers] for program in programs]
        warm_before = [(spread_scale,), (turn, "k", 0), (turn, "q", 2), (first_projection, "k", 0, 0)]
        written = []
        banks = {}
        at, read, filled = [0, 0], [0, 0], [0, 0]

        def fill_ahead(e):
            for step in with_bank[e][filled[e] : read[e] + AHEAD]:
                if not all(need in written for need in bank_needs(step)):
                    return
                if step in warm_before:
                    warm_up()
                banks[step] = fillers[step[0]](*step[1:])
                filled[e] = filled[e] + 1

        for visit in range(2 * (len(on_vector) + len(on_scalar))):
            e = visit % 2
            if at[e] < len(programs[e]) and all(need in written for need in needs(programs[e][at[e]])):
                step = programs[e][at[e]]
                at[e] = at[e] + 1
                fill_ahead(0)
                fill_ahead(1)
                if step[0] in fillers:
                    step[0](banks[step], *step[1:])
                    read[e] = read[e] + 1
                else:
                    step[0](*step[1:])
                written.extend(makes(step))
        assert at == [len(on_vector), len(on_scalar)]
